import numpy as np
import ml_dtypes


def mxq(x, axis, fmt="e4m3"):
    dtype, down = {"e4m3": (ml_dtypes.float8_e4m3fn, 7), "e5m2": (ml_dtypes.float8_e5m2, 14)}[fmt]
    v = np.moveaxis(np.asarray(x, np.float32).astype(ml_dtypes.bfloat16).astype(np.float64), axis, -1)
    blocks = v.reshape(v.shape[:-1] + (-1, 32))
    amax = np.abs(blocks).max(-1, keepdims=True)
    byte = np.maximum(np.where(amax > 0, np.frexp(amax)[1] - 1 + 127, 0) - down, 1)
    scale = np.exp2(byte - 127.0)
    codes = (blocks / scale).astype(np.float32).astype(dtype).astype(np.float64)
    return np.moveaxis((codes * scale).reshape(v.shape), -1, axis)


WIDE = False


def mx_kscale(k):
    if not WIDE:
        return np.ones(k)
    levels = np.array([10, -10, 5, -5, 0])
    if k % 512:
        return np.exp2(np.random.permutation(np.resize(levels, k // 32))).repeat(32)
    a = np.empty((k // 512, 16))
    for p in range(k // 512):
        a[p, :8] = np.random.permutation(np.resize(levels, 8))
        for g in range(8):
            far = levels[np.abs(levels - a[p, g]) >= 10]
            a[p, g + 8] = far[np.random.randint(len(far))]
    return np.exp2(a.ravel()).repeat(32)


def f64(x):
    return np.asarray(x).astype(np.float64)


def striped(idx):
    return np.tile(idx.reshape(-1, 16).T, (8, 1)).astype(np.uint16)


def unstriped(offs):
    return offs[:16].T.reshape(-1).astype(np.int64)


E2M1 = np.array([0.0, 0.5, 1.0, 1.5, 2.0, 3.0, 4.0, 6.0, -0.0, -0.5, -1.0, -1.5, -2.0, -3.0, -4.0, -6.0])


def pack_weight(w, fmt):
    k, n = w.shape
    w = f64(np.asarray(w, np.float32).astype(ml_dtypes.bfloat16)).reshape(k // 32, 32, n)
    amax = np.abs(w).max(1)
    if fmt == "e4m3":
        byte = np.frexp(amax)[1] - 1 + 127 - 7
    else:
        mant, ex = np.frexp(amax / 6.0)
        byte = np.where(mant > 0.5, ex, ex - 1) + 127
    byte = np.clip(np.where(amax > 0, byte, 1), 1, 254)
    scaled = (w * np.exp2(127.0 - byte)[:, None, :]).reshape(k, n).astype(np.float32)
    by_word = np.ascontiguousarray(scaled.reshape(k // 512, 128, 4, n).transpose(0, 1, 3, 2))
    if fmt == "e4m3":
        words = by_word.astype(ml_dtypes.float8_e4m3fn).view(np.uint8)
    else:
        c = by_word.astype(ml_dtypes.float4_e2m1fn).view(np.uint8) & 0xF
        words = (c[..., 0::2] | (c[..., 1::2] << 4)).reshape(k // 512, 128, 2 * n)
    return np.ascontiguousarray(words), np.ascontiguousarray(byte.astype(np.uint8).reshape(k // 512, 16, n))


def unpack_weight(words, scales, fmt):
    g, _, n = scales.shape
    words = np.ascontiguousarray(words).reshape(g, 128, n, -1)
    if fmt == "e4m3":
        vals = words.view(ml_dtypes.float8_e4m3fn).astype(np.float64)
    else:
        nib = np.empty((g, 128, n, 4), np.uint8)
        nib[..., 0::2] = words & 0xF
        nib[..., 1::2] = words >> 4
        vals = E2M1[nib]
    vals = vals * np.repeat(np.exp2(scales.astype(np.float64) - 127.0), 8, axis=1)[..., None]
    return vals.transpose(0, 1, 3, 2).reshape(g * 512, n)


def gelu(v):
    return 0.5 * v * (1.0 + np.tanh(np.sqrt(2.0 / np.pi) * (v + 0.044715 * v**3)))


K, H, N, T, TB, S, T2, P = 1024, 1024, 512, 2048, 1024, 512, 2048, 1024

def setup_inputs():
    n = np.random.standard_normal
    s = mx_kscale(K)[:, None]
    u = mx_kscale(H)[:, None]
    d = {}
    d["tab_words"], d["tab_scales"] = pack_weight(n((K, T)) * s, "e4m3")
    d["tab2_words"], d["tab2_scales"] = pack_weight(n((K, TB)) * s, "e4m3")
    d["offs"] = striped(np.random.permutation(T)[:S])
    d["offs2"] = striped(np.random.permutation(TB)[:S])
    perm = np.random.permutation(T2)
    d["offs3"] = striped(perm[:S])
    d["offs4"] = striped(perm[S:2 * S])
    d["offs5"] = striped(np.random.permutation(T2)[:P])
    d["w1"] = (n((K, H)) / s / K ** 0.5).astype(np.float32)
    d["w2_words"], d["w2_scales"] = pack_weight(1.6 * n((K, H)) / s / K ** 0.5, "e2m1")
    d["w3"] = (n((H, H)) / u * u.T / H ** 0.5).astype(np.float32)
    d["w4_words"], d["w4_scales"] = pack_weight(1.2 * n((H, N)) / u / H ** 0.5, "e4m3")
    d["sg"] = (0.6 * np.exp(0.3 * n(H)) * u[:, 0]).astype(np.float32)
    d["fg"] = (np.exp(0.3 * n(H)) * u[:, 0]).astype(np.float32)
    d["pv"] = (0.7 * n(H) * u[:, 0]).astype(np.float32)
    d["wg1"] = np.exp(0.3 * n((128, S))).astype(np.float32)
    d["wg2"] = np.exp(0.3 * n((128, S))).astype(np.float32)
    d["page0"] = (n((H, T2)) * u).astype(np.float32)
    return d

def reference(tab_words, tab_scales, tab2_words, tab2_scales, offs, offs2, offs3, offs4, offs5,
              w1, w2_words, w2_scales, w3, w4_words, w4_scales, sg, fg, pv, wg1, wg2, page0):
    v = unpack_weight(tab_words, tab_scales, "e4m3")[:, unstriped(offs)]
    v2 = unpack_weight(tab2_words, tab2_scales, "e4m3")[:, unstriped(offs2)]
    sp = mxq(f64(w1), 0, "e4m3").T @ v
    h1 = f64(sg)[:, None] * np.square(sp)
    f = unpack_weight(w2_words, w2_scales, "e2m1").T @ v2
    tf = f64(fg)[:, None] * np.tanh(f)
    h2 = (mxq(f64(w3), 0, "e4m3").T @ mxq(tf, 0, "e4m3")) * f
    page = f64(page0).copy()
    page[:, unstriped(offs3)] = np.tile(f64(wg1), (H // 128, 1)) * h1
    page[:, unstriped(offs4)] = np.tile(f64(wg2), (H // 128, 1)) * h2
    x = page[:, unstriped(offs5)] + f64(pv)[:, None]
    y = unpack_weight(w4_words, w4_scales, "e4m3").T @ mxq(x, 0, "e4m3")
    return 0.5 * y * (1.0 + np.tanh(0.7978845608028654 * (y + 0.044715 * y ** 3)))

@@ -1,0 +1,303 @@
+from contextlib import ExitStack
+
+import concourse.mybir as mybir
+
+K, H, N, T, TB, S, T2, PJ = 1024, 1024, 512, 2048, 1024, 512, 2048, 1024
+FLOPS = 2 * (K * H * S * 2 + H * H * S + H * N * PJ)
+
+F32 = mybir.dt.float32
+BF16 = mybir.dt.bfloat16
+I32 = mybir.dt.int32
+U32 = mybir.dt.uint32
+U16 = mybir.dt.uint16
+U8 = mybir.dt.uint8
+FP8X4 = mybir.dt.float8_e4m3fn_x4
+FP4X4 = mybir.dt.float4_e2m1fn_x4
+ACT = mybir.ActivationFunctionType
+MULT = mybir.AluOpType.mult
+
+P = 128
+PACK = 4
+KP = P * PACK
+CH = 256
+
+
+def tile_list_contact_wire_slots_kernel(
+    tc, tab_words, tab_scales, tab2_words, tab2_scales, offs, offs2, offs3, offs4, offs5,
+    w1, w2_words, w2_scales, w3, w4_words, w4_scales, sg, fg, pv, wg1, wg2, page0, out,
+):
+    nc = tc.nc
+    with ExitStack() as ctx:
+        keep = ctx.enter_context(tc.tile_pool(name="keep", bufs=1))
+        work = ctx.enter_context(tc.tile_pool(name="work", bufs=1))
+        psum = ctx.enter_context(tc.psum_pool(name="psum", bufs=1))
+
+        def held(shape, dtype, name):
+            return keep.tile(shape, dtype, name=name, align_bytes=64)
+
+        def ring(shape, dtype, tag, bufs):
+            return work.tile(shape, dtype, name=tag, tag=tag, bufs=bufs, align_bytes=64)
+
+        def load_list(src, name):
+            t = keep.tile(list(src.shape), U16, name=name)
+            nc.sync.dma_start(t[:], src)
+            return t
+
+        def load_words(src, tag, bufs):
+            t = ring([P, src.shape[1]], I32, tag, bufs)
+            nc.sync.dma_start(t[:], src.rearrange("p t i -> p (t i)").bitcast(I32))
+            return t
+
+        def load_planes(src, name, eng, clear):
+            t = held([P, 2, src.shape[2]], U8, name)
+            clear.memset(t[:].bitcast(I32), 0)
+            for q in range(4):
+                eng.dma_start(
+                    t[32 * q : 32 * q + 4, :, :].bitcast(I32),
+                    src[:, 4 * q : 4 * q + 4, :].rearrange("a r c -> r a c").bitcast(I32),
+                )
+            return t
+
+        def load_vec(src, name):
+            t = held([P, 2, PACK], F32, name)
+            nc.sync.dma_start(t[:], src.rearrange("(b p t) -> p b t", b=2, t=PACK))
+            return t
+
+        def load_w(src, a, b, tag):
+            t = ring([P, PACK, KP], F32, tag, 1)
+            nc.sync.dma_start(
+                t[:], src[KP * a : KP * (a + 1), KP * b : KP * (b + 1)].rearrange("(p j) c -> p j c", j=PACK)
+            )
+            return t
+
+        def load_page(b, t, tag):
+            pg = ring([P, T2], F32, tag, 1)
+            nc.sync.dma_start(pg[:], page0.rearrange("(b p t) s -> b t p s", b=2, t=PACK)[b, t])
+            return pg
+
+        def load_wg(src, name):
+            t = held([P, PACK, S], F32, name)
+            rows = src.rearrange("(q t) s -> q t s", t=PACK)
+            for q in (0, 2, 1, 3):
+                nc.sync.dma_start(t[32 * q : 32 * q + 32, :, :], rows)
+            return t
+
+        def quantize(src, width, tag, bufs):
+            codes = ring([P, width], U32, tag + "_codes", bufs)
+            scales = ring([P, width], U8, tag + "_scales", bufs)
+            nc.vector.quantize_mx(out=codes[:].bitcast(FP8X4), scales=scales[:], in_=src)
+            return codes, scales
+
+        def quantize_w(raw, tag):
+            wb = ring([P, PACK * KP], BF16, "grouped", 3)
+            nc.scalar.copy(
+                wb[:].rearrange("p (t m j) -> p m j t", t=PACK, j=PACK),
+                raw[:].rearrange("p j (m t) -> p m j t", t=PACK),
+            )
+            return quantize(wb[:], KP, tag, 4)
+
+        def interleave(eng_copy, planes, c0, width):
+            g = ring([P, PACK * width], BF16, "grouped", 3)
+            eng_copy(
+                g[:].rearrange("p (c i t) -> p c t i", i=4, t=PACK),
+                planes[:, :, c0 : c0 + width].rearrange("p t (c i) -> p c t i", i=4),
+            )
+            return g
+
+        warm = held([P, 2], F32, "warm")
+        nc.gpsimd.memset(warm[:, 0:1], 0.0)
+        nc.scalar.activation(warm[:, 1:2], warm[:, 0:1], ACT.Gelu_apprx_tanh)
+        tab2w, tabw, w1raw, w3raw, pages = {}, {}, {}, {}, {}
+        o2 = load_list(offs2, "o2")
+        tab2w[0] = load_words(tab2_words[0], "k4", 3)
+        w2raw = ring([P, 2, 2 * H], U8, "k4", 3)
+        nc.sync.dma_start(w2raw[:].bitcast(I32), w2_words.rearrange("a p c -> p a c").bitcast(I32))
+        tab2w[1] = load_words(tab2_words[1], "k4", 3)
+        w2sraw = load_planes(w2_scales, "w2sraw", nc.sync, nc.gpsimd)
+        w1raw[0, 0] = load_w(w1, 0, 0, "s0")
+        tab2s = load_planes(tab2_scales, "tab2s", nc.sync, nc.vector)
+        w1raw[1, 0] = load_w(w1, 1, 0, "s1")
+        fgt = load_vec(fg, "fgt")
+        o1 = load_list(offs, "o1")
+        tabw[0] = load_words(tab_words[0], "s2", 1)
+        tabs = held([P, T], U8, "tabs")
+        nc.gpsimd.memset(tabs[:].bitcast(I32), 0)
+        for q in range(4):
+            nc.sync.dma_start(
+                tabs[32 * q : 32 * q + 8, :].bitcast(I32), tab_scales[:, 4 * q : 4 * q + 4, :].bitcast(I32)
+            )
+        tabw[1] = load_words(tab_words[1], "s3", 1)
+        wg2t = load_wg(wg2, "wg2t")
+        o3 = load_list(offs3, "o3")
+        sgt = load_vec(sg, "sgt")
+        wg1t = load_wg(wg1, "wg1t")
+        pages[0, 0] = load_page(0, 0, "s4")
+        w3raw[0, 0] = load_w(w3, 0, 0, "s5")
+        w3raw[1, 0] = load_w(w3, 1, 0, "s7")
+        o4 = load_list(offs4, "o4")
+        pages[0, 1] = load_page(0, 1, "s6")
+        o5 = load_list(offs5, "o5")
+        pvt = load_vec(pv, "pvt")
+        pages[0, 2] = load_page(0, 2, "s8")
+        w4s = load_planes(w4_scales, "w4s", nc.sync, nc.vector)
+        w1raw[0, 1] = load_w(w1, 0, 1, "s9")
+        w4w = [load_words(w4_words[a], "w4w", 2) for a in range(2)]
+
+        v2 = [held([P, S], U32, "v2_%d" % a) for a in range(2)]
+        v2s = [held([P, S], U8, "v2s_%d" % a) for a in range(2)]
+        w2p = [held([P, 2 * H], U8, "w2p_%d" % a) for a in range(2)]
+        w2sp = held([P, 2, H], U8, "w2sp")
+        for a in range(2):
+            nc.vector.tensor_copy(v2[a][:], tab2w[a][:].bitcast(U32).indirect(o2[:]))
+            nc.vector.tensor_copy(
+                w2p[a][:].bitcast(U16).rearrange("p (b t q) -> p b t q", b=2, t=PACK),
+                w2raw[:, a, :].bitcast(U16).rearrange("p (b q t) -> p b t q", b=2, t=PACK),
+            )
+            nc.vector.tensor_copy(v2s[a][:], tab2s[:, a, :].indirect(o2[:]))
+        nc.vector.tensor_copy(
+            w2sp[:].rearrange("p a (b t q) -> p (a b) t q", b=2, t=PACK),
+            w2sraw[:].rearrange("p a (b q t) -> p (a b) t q", b=2, t=PACK),
+        )
+
+        w1q = {(a, 0): quantize_w(w1raw[a, 0], "w1") for a in range(2)}
+        v = [held([P, S], U32, "v_%d" % a) for a in range(2)]
+        vs = held([P, S], U8, "vs")
+        nc.vector.tensor_copy(vs[:], tabs[:].indirect(o1[:]))
+        for a in range(2):
+            nc.vector.tensor_copy(v[a][:], tabw[a][:].bitcast(U32).indirect(o1[:]))
+
+        w1raw[1, 1] = load_w(w1, 1, 1, "s0")
+        w3raw[0, 1] = load_w(w3, 0, 1, "s1")
+        w3raw[1, 1] = load_w(w3, 1, 1, "s2")
+        pages[0, 3] = load_page(0, 3, "s3")
+
+        h1 = {}
+
+        def make_h1(b, t):
+            acc = psum.tile([P, S], F32, name="acc_b", tag="acc_b", bufs=2)
+            for a in range(2):
+                codes, scales = w1q[a, b]
+                nc.tensor.matmul_mx(
+                    out=acc[:], lhsT=codes[:, P * t : P * (t + 1)].bitcast(FP8X4),
+                    lhsT_scale=scales[:, P * t : P * (t + 1)],
+                    rhs=v[a][:].bitcast(FP8X4), rhs_scale=vs[4 * a : P, :], start=(a == 0), stop=(a == 1),
+                )
+            gain = ring([P, S], F32, "gain", 2)
+            nc.scalar.activation(gain[:], wg1t[:, t, :], ACT.Copy, scale=sgt[:, b, t : t + 1])
+            sq = ring([P, S], F32, "sq", 2)
+            nc.scalar.activation(sq[:], acc[:], ACT.Square)
+            h1[b, t] = (sq, gain)
+
+        def put_h1(b, t):
+            sq, gain = h1[b, t]
+            nc.vector.tensor_tensor(pages[b, t][:].indirect(o3[:]), sq[:], gain[:], MULT)
+
+        make_h1(0, 0)
+        put_h1(0, 0)
+
+        fw = {}
+        tfq = []
+        tfp = ring([P, 2, PACK, S], BF16, "planes", 1)
+        for b in range(2):
+            for t in range(PACK):
+                acc = psum.tile([P, S], F32, name="acc_a", tag="acc_a", bufs=6)
+                c0 = KP * b + P * t
+                for a in range(2):
+                    nc.tensor.matmul_mx(
+                        out=acc[:], lhsT=w2p[a][:, 2 * c0 : 2 * (c0 + P)].bitcast(FP4X4),
+                        lhsT_scale=w2sp[:, a, c0 : c0 + P],
+                        rhs=v2[a][:].bitcast(FP8X4), rhs_scale=v2s[a][:], start=(a == 0), stop=(a == 1),
+                    )
+                th = ring([P, S], F32, "th", 2)
+                nc.scalar.activation(th[:], acc[:], ACT.Tanh)
+                fw[b, t] = held([P, S], F32, "fw_%d_%d" % (b, t))
+                nc.vector.tensor_tensor(fw[b, t][:], acc[:], wg2t[:, t, :], MULT)
+                nc.scalar.activation(tfp[:, b, t, :], th[:], ACT.Copy, scale=fgt[:, b, t : t + 1])
+            tfq.append(quantize(interleave(nc.vector.tensor_copy, tfp[:, b], 0, S)[:], S, "tf", 2))
+            if b == 0:
+                make_h1(0, 1)
+                put_h1(0, 1)
+
+        g = {}
+
+        def make_g(b, t):
+            acc = psum.tile([P, S], F32, name="acc_b", tag="acc_b", bufs=2)
+            for a in range(2):
+                codes, scales = w3q[a, b]
+                nc.tensor.matmul_mx(
+                    out=acc[:], lhsT=codes[:, P * t : P * (t + 1)].bitcast(FP8X4),
+                    lhsT_scale=scales[:, P * t : P * (t + 1)],
+                    rhs=tfq[a][0][:].bitcast(FP8X4), rhs_scale=tfq[a][1][:], start=(a == 0), stop=(a == 1),
+                )
+            g[b, t] = ring([P, S], F32, "g", 2)
+            nc.scalar.copy(g[b, t][:], acc[:])
+
+        def put_h2(b, t):
+            nc.vector.tensor_tensor(pages[b, t][:].indirect(o4[:]), g[b, t][:], fw[b, t][:], MULT)
+
+        w3q = {(a, 0): quantize_w(w3raw[a, 0], "w3") for a in range(2)}
+        pages[1, 0] = load_page(1, 0, "s5")
+        pages[1, 1] = load_page(1, 1, "s7")
+        make_g(0, 0)
+        make_h1(0, 2)
+        make_g(0, 1)
+        put_h1(0, 2)
+        make_h1(0, 3)
+        for a in range(2):
+            w1q[a, 1] = quantize_w(w1raw[a, 1], "w1")
+        pages[1, 2] = load_page(1, 2, "s9")
+        pages[1, 3] = load_page(1, 3, "s0")
+        make_h1(1, 0)
+        for a in range(2):
+            w3q[a, 1] = quantize_w(w3raw[a, 1], "w3")
+
+        def fetch(b, t, planes, c0, width, tag, bufs):
+            xg = ring([P, width], F32, tag, bufs)
+            nc.vector.tensor_copy(xg[:], pages[b, t][:].indirect(o5[:, c0 // 16 : (c0 + width) // 16]))
+            nc.scalar.activation(planes[:, t, c0 : c0 + width], xg[:], ACT.Identity, bias=pvt[:, b, t : t + 1])
+
+        xp0 = ring([P, PACK, PJ], BF16, "s2", 1)
+        for t in range(PACK):
+            if t == 3:
+                put_h1(0, 3)
+                make_h1(1, 1)
+            put_h2(0, t)
+            make_g(*divmod(t + 2, PACK))
+            fetch(0, t, xp0, 0, PJ, "k4", 3)
+
+        xp1 = ring([P, PACK, PJ], BF16, "planes", 1)
+        xq0 = []
+        for t in range(PACK):
+            put_h1(1, t)
+            if t < 2:
+                make_h1(1, t + 2)
+            put_h2(1, t)
+            if t < 2:
+                make_g(1, t + 2)
+                xq0.append(quantize(interleave(nc.scalar.copy, xp0, S * t, S)[:], S, "x0", 2))
+            if t < PACK - 1:
+                fetch(1, t, xp1, 0, PJ, "k4", 3)
+
+        fetch(1, PACK - 1, xp1, 0, CH, "xlast", 2)
+        for c in range(PJ // CH):
+            if c + 1 < PJ // CH:
+                fetch(1, PACK - 1, xp1, CH * (c + 1), CH, "xlast", 2)
+            xq1 = quantize(interleave(nc.vector.tensor_copy, xp1, CH * c, CH)[:], CH, "x1", 4)
+            h, cc = divmod(CH * c, S)
+            rhs = [(xq0[h][0][:, cc : cc + CH], xq0[h][1][:, cc : cc + CH]), (xq1[0][:], xq1[1][:])]
+            for n2 in range(2):
+                acc = psum.tile([P, 2, CH], F32, name="acc_a", tag="acc_a", bufs=6)
+                for nn in range(2):
+                    n0 = P * (2 * n2 + nn)
+                    for a in range(2):
+                        nc.tensor.matmul_mx(
+                            out=acc[:, nn, :], lhsT=w4w[a][:, n0 : n0 + P].bitcast(FP8X4),
+                            lhsT_scale=w4s[:, a, n0 : n0 + P],
+                            rhs=rhs[a][0].bitcast(FP8X4), rhs_scale=rhs[a][1], start=(a == 0), stop=(a == 1),
+                        )
+                res = ring([P, 2, CH], F32, "res", 6)
+                nc.scalar.activation(res[:], acc[:], ACT.Gelu_apprx_tanh)
+                nc.sync.dma_start(
+                    out[2 * P * n2 : 2 * P * (n2 + 1), CH * c : CH * (c + 1)].rearrange("(n p) j -> p n j", p=P),
+                    res[:],
+                )

@@ -75,31 +75,32 @@ def tile_list_contact_wire_slots_kernel(
             nc.sync.dma_start(pg[:], page0.rearrange("(b p t) s -> b t p s", b=2, t=PACK)[b, t])
             return pg
 
-        def load_wg(src, name):
-            t = held([P, PACK, S], F32, name)
-            rows = src.rearrange("(q t) s -> q t s", t=PACK)
+        def load_wg(src, u, name):
+            t = held([P, 2, S], F32, name)
+            rows = src.rearrange("(q t) s -> q t s", t=PACK)[:, 2 * u : 2 * u + 2, :]
             for q in (0, 2, 1, 3):
                 nc.sync.dma_start(t[32 * q : 32 * q + 32, :, :], rows)
             return t
 
-        def quantize(src, width, tag, bufs):
-            codes = ring([P, width], U32, tag + "_codes", bufs)
+        def quantize(src, width, tag, bufs, codes_in=None):
+            codes = ring([P, width], U32, codes_in or tag + "_codes", 1 if codes_in else bufs)
             scales = ring([P, width], U8, tag + "_scales", bufs)
             nc.vector.quantize_mx(out=codes[:].bitcast(FP8X4), scales=scales[:], in_=src)
             return codes, scales
 
         def quantize_w(raw, tag):
-            wb = ring([P, PACK * KP], BF16, "grouped", 3)
+            wb = ring([P, PACK * KP], BF16, "grouped", 4)
             nc.scalar.copy(
                 wb[:].rearrange("p (t m j) -> p m j t", t=PACK, j=PACK),
                 raw[:].rearrange("p j (m t) -> p m j t", t=PACK),
             )
             return quantize(wb[:], KP, tag, 4)
 
-        def interleave(eng_copy, planes, c0, width):
-            g = ring([P, PACK * width], BF16, "grouped", 3)
+        def interleave(eng_copy, planes, c0, width, g=None):
+            if g is None:
+                g = ring([P, PACK * width], BF16, "grouped", 4)[:]
             eng_copy(
-                g[:].rearrange("p (c i t) -> p c t i", i=4, t=PACK),
+                g.rearrange("p (c i t) -> p c t i", i=4, t=PACK),
                 planes[:, :, c0 : c0 + width].rearrange("p t (c i) -> p c t i", i=4),
             )
             return g
@@ -113,10 +114,10 @@ def tile_list_contact_wire_slots_kernel(
         w2raw = ring([P, 2, 2 * H], U8, "k4", 3)
         nc.sync.dma_start(w2raw[:].bitcast(I32), w2_words.rearrange("a p c -> p a c").bitcast(I32))
         tab2w[1] = load_words(tab2_words[1], "k4", 3)
-        w2sraw = load_planes(w2_scales, "w2sraw", nc.sync, nc.gpsimd)
         w1raw[0, 0] = load_w(w1, 0, 0, "s0")
-        tab2s = load_planes(tab2_scales, "tab2s", nc.sync, nc.vector)
+        tab2s = load_planes(tab2_scales, "tab2s", nc.sync, nc.gpsimd)
         w1raw[1, 0] = load_w(w1, 1, 0, "s1")
+        w2sraw = load_planes(w2_scales, "w2sraw", nc.sync, nc.vector)
         fgt = load_vec(fg, "fgt")
         o1 = load_list(offs, "o1")
         tabw[0] = load_words(tab_words[0], "s2", 1)
@@ -127,23 +128,24 @@ def tile_list_contact_wire_slots_kernel(
                 tabs[32 * q : 32 * q + 8, :].bitcast(I32), tab_scales[:, 4 * q : 4 * q + 4, :].bitcast(I32)
             )
         tabw[1] = load_words(tab_words[1], "s3", 1)
-        wg2t = load_wg(wg2, "wg2t")
+        wg2t = {0: load_wg(wg2, 0, "wg2_0")}
         o3 = load_list(offs3, "o3")
         sgt = load_vec(sg, "sgt")
-        wg1t = load_wg(wg1, "wg1t")
+        wg1t = {0: load_wg(wg1, 0, "wg1_0")}
         pages[0, 0] = load_page(0, 0, "s4")
         w3raw[0, 0] = load_w(w3, 0, 0, "s5")
         w3raw[1, 0] = load_w(w3, 1, 0, "s7")
-        o4 = load_list(offs4, "o4")
         pages[0, 1] = load_page(0, 1, "s6")
+        o4 = load_list(offs4, "o4")
         o5 = load_list(offs5, "o5")
         pvt = load_vec(pv, "pvt")
-        pages[0, 2] = load_page(0, 2, "s8")
-        w4s = load_planes(w4_scales, "w4s", nc.sync, nc.vector)
+        wg1t[1] = load_wg(wg1, 1, "wg1_1")
         w1raw[0, 1] = load_w(w1, 0, 1, "s9")
-        w4w = [load_words(w4_words[a], "w4w", 2) for a in range(2)]
+        wg2t[1] = load_wg(wg2, 1, "wg2_1")
+        w1raw[1, 1] = load_w(w1, 1, 1, "s8")
+        w4s = load_planes(w4_scales, "w4s", nc.sync, nc.gpsimd)
 
-        v2 = [held([P, S], U32, "v2_%d" % a) for a in range(2)]
+        v2 = [ring([P, S], U32, "v2", 2) for a in range(2)]
         v2s = [held([P, S], U8, "v2s_%d" % a) for a in range(2)]
         w2p = [held([P, 2 * H], U8, "w2p_%d" % a) for a in range(2)]
         w2sp = held([P, 2, H], U8, "w2sp")
@@ -166,12 +168,12 @@ def tile_list_contact_wire_slots_kernel(
         for a in range(2):
             nc.vector.tensor_copy(v[a][:], tabw[a][:].bitcast(U32).indirect(o1[:]))
 
-        w1raw[1, 1] = load_w(w1, 1, 1, "s0")
-        w3raw[0, 1] = load_w(w3, 0, 1, "s1")
-        w3raw[1, 1] = load_w(w3, 1, 1, "s2")
-        pages[0, 3] = load_page(0, 3, "s3")
+        w3raw[0, 1] = load_w(w3, 0, 1, "s0")
+        w3raw[1, 1] = load_w(w3, 1, 1, "s1")
+        pages[0, 2] = load_page(0, 2, "s2")
 
         h1 = {}
+        sq1 = []
 
         def make_h1(b, t):
             acc = psum.tile([P, S], F32, name="acc_b", tag="acc_b", bufs=2)
@@ -182,21 +184,20 @@ def tile_list_contact_wire_slots_kernel(
                     lhsT_scale=scales[:, P * t : P * (t + 1)],
                     rhs=v[a][:].bitcast(FP8X4), rhs_scale=vs[4 * a : P, :], start=(a == 0), stop=(a == 1),
                 )
-            gain = ring([P, S], F32, "gain", 2)
-            nc.scalar.activation(gain[:], wg1t[:, t, :], ACT.Copy, scale=sgt[:, b, t : t + 1])
-            sq = ring([P, S], F32, "sq", 2)
-            nc.scalar.activation(sq[:], acc[:], ACT.Square)
-            h1[b, t] = (sq, gain)
+            sq = ring([P, S], F32, "sq", 4)[:] if b == 0 else sq1[0][:, t, :]
+            nc.scalar.activation(sq, acc[:], ACT.Square)
+            nc.scalar.activation(sq, sq, ACT.Copy, scale=sgt[:, b, t : t + 1])
+            h1[b, t] = sq
 
         def put_h1(b, t):
-            sq, gain = h1[b, t]
-            nc.vector.tensor_tensor(pages[b, t][:].indirect(o3[:]), sq[:], gain[:], MULT)
+            nc.vector.tensor_tensor(pages[b, t][:].indirect(o3[:]), h1[b, t], wg1t[t // 2][:, t % 2, :], MULT)
 
         make_h1(0, 0)
         put_h1(0, 0)
 
         fw = {}
         tfq = []
+        tfg = ring([P, 2, PACK * S], BF16, "s3", 1)
         tfp = ring([P, 2, PACK, S], BF16, "planes", 1)
         for b in range(2):
             for t in range(PACK):
@@ -210,14 +211,16 @@ def tile_list_contact_wire_slots_kernel(
                     )
                 th = ring([P, S], F32, "th", 2)
                 nc.scalar.activation(th[:], acc[:], ACT.Tanh)
-                fw[b, t] = held([P, S], F32, "fw_%d_%d" % (b, t))
-                nc.vector.tensor_tensor(fw[b, t][:], acc[:], wg2t[:, t, :], MULT)
+                fw[b, t] = ring([P, S], F32, "fw_%d_%d" % (b, t), 1)
+                nc.vector.tensor_tensor(fw[b, t][:], acc[:], wg2t[t // 2][:, t % 2, :], MULT)
                 nc.scalar.activation(tfp[:, b, t, :], th[:], ACT.Copy, scale=fgt[:, b, t : t + 1])
-            tfq.append(quantize(interleave(nc.vector.tensor_copy, tfp[:, b], 0, S)[:], S, "tf", 2))
+            tfq.append(quantize(interleave(nc.vector.tensor_copy, tfp[:, b], 0, S, tfg[:, b, :]), S, "tf", 2))
             if b == 0:
                 make_h1(0, 1)
                 put_h1(0, 1)
 
+        pages[0, 3] = load_page(0, 3, "s3")
+        w4w = [load_words(w4_words[a], "v2", 2) for a in range(2)]
         g = {}
 
         def make_g(b, t):
@@ -229,7 +232,7 @@ def tile_list_contact_wire_slots_kernel(
                     lhsT_scale=scales[:, P * t : P * (t + 1)],
                     rhs=tfq[a][0][:].bitcast(FP8X4), rhs_scale=tfq[a][1][:], start=(a == 0), stop=(a == 1),
                 )
-            g[b, t] = ring([P, S], F32, "g", 2)
+            g[b, t] = ring([P, S], F32, "g", 4)
             nc.scalar.copy(g[b, t][:], acc[:])
 
         def put_h2(b, t):
@@ -238,65 +241,78 @@ def tile_list_contact_wire_slots_kernel(
         w3q = {(a, 0): quantize_w(w3raw[a, 0], "w3") for a in range(2)}
         pages[1, 0] = load_page(1, 0, "s5")
         pages[1, 1] = load_page(1, 1, "s7")
-        make_g(0, 0)
+        for t in range(PACK):
+            make_g(0, t)
         make_h1(0, 2)
-        make_g(0, 1)
-        put_h1(0, 2)
         make_h1(0, 3)
         for a in range(2):
             w1q[a, 1] = quantize_w(w1raw[a, 1], "w1")
         pages[1, 2] = load_page(1, 2, "s9")
-        pages[1, 3] = load_page(1, 3, "s0")
-        make_h1(1, 0)
+        pages[1, 3] = load_page(1, 3, "s8")
         for a in range(2):
             w3q[a, 1] = quantize_w(w3raw[a, 1], "w3")
+        sq1.append(ring([P, PACK, S], F32, "s1", 1))
+        for t in range(PACK):
+            make_h1(1, t)
 
         def fetch(b, t, planes, c0, width, tag, bufs):
             xg = ring([P, width], F32, tag, bufs)
             nc.vector.tensor_copy(xg[:], pages[b, t][:].indirect(o5[:, c0 // 16 : (c0 + width) // 16]))
             nc.scalar.activation(planes[:, t, c0 : c0 + width], xg[:], ACT.Identity, bias=pvt[:, b, t : t + 1])
 
-        xp0 = ring([P, PACK, PJ], BF16, "s2", 1)
+        xp0 = ring([P, PACK, PJ], BF16, "s0", 1)
         for t in range(PACK):
-            if t == 3:
-                put_h1(0, 3)
-                make_h1(1, 1)
+            if t >= 2:
+                put_h1(0, t)
             put_h2(0, t)
-            make_g(*divmod(t + 2, PACK))
+            make_g(1, t)
             fetch(0, t, xp0, 0, PJ, "k4", 3)
 
-        xp1 = ring([P, PACK, PJ], BF16, "planes", 1)
-        xq0 = []
+        x0g = [interleave(nc.scalar.copy, xp0, S * h, S) for h in range(2)]
+        xp1 = ring([P, PACK, PJ], BF16, "s0", 1)
+        acc_y = {}
+
+        def y_pass(a, c, codes, scales):
+            for n in range(N // P):
+                n2, nn = divmod(n, 2)
+                nc.tensor.matmul_mx(
+                    out=acc_y[c, n2][:, nn, :], lhsT=w4w[a][:, P * n : P * (n + 1)].bitcast(FP8X4),
+                    lhsT_scale=w4s[:, a, P * n : P * (n + 1)],
+                    rhs=codes.bitcast(FP8X4), rhs_scale=scales,
+                    start=(a == 0 and nn == 0), stop=(a == 1 and nn == 1),
+                )
+
         for t in range(PACK):
             put_h1(1, t)
-            if t < 2:
-                make_h1(1, t + 2)
             put_h2(1, t)
             if t < 2:
-                make_g(1, t + 2)
-                xq0.append(quantize(interleave(nc.scalar.copy, xp0, S * t, S)[:], S, "x0", 2))
+                codes, scales = quantize(x0g[t], S, "x0", 2, "fw_1_%d" % t)
+                for cc in range(S // CH):
+                    c = (S // CH) * t + cc
+                    for n2 in range(2):
+                        last = c == PJ // CH - 1
+                        acc_y[c, n2] = psum.tile(
+                            [P, 2, CH], F32, name="acc_y", tag="acc_b" if last else "acc_a", bufs=2 if last else 6
+                        )
+                    y_pass(0, c, codes[:, CH * cc : CH * (cc + 1)], scales[:, CH * cc : CH * (cc + 1)])
             if t < PACK - 1:
                 fetch(1, t, xp1, 0, PJ, "k4", 3)
 
-        fetch(1, PACK - 1, xp1, 0, CH, "xlast", 2)
+        for h in range(2):
+            xg = ring([P, S], F32, "k4", 3)
+            nc.vector.tensor_copy(xg[:], pages[1, PACK - 1][:].indirect(o5[:, S * h // 16 : S * (h + 1) // 16]))
+            for cc in range(S // CH):
+                c0 = S * h + CH * cc
+                nc.scalar.activation(
+                    xp1[:, PACK - 1, c0 : c0 + CH], xg[:, CH * cc : CH * (cc + 1)], ACT.Identity,
+                    bias=pvt[:, 1, PACK - 1 : PACK],
+                )
         for c in range(PJ // CH):
-            if c + 1 < PJ // CH:
-                fetch(1, PACK - 1, xp1, CH * (c + 1), CH, "xlast", 2)
-            xq1 = quantize(interleave(nc.vector.tensor_copy, xp1, CH * c, CH)[:], CH, "x1", 4)
-            h, cc = divmod(CH * c, S)
-            rhs = [(xq0[h][0][:, cc : cc + CH], xq0[h][1][:, cc : cc + CH]), (xq1[0][:], xq1[1][:])]
+            codes, scales = quantize(interleave(nc.vector.tensor_copy, xp1, CH * c, CH), CH, "x1", 4)
+            y_pass(1, c, codes[:], scales[:])
             for n2 in range(2):
-                acc = psum.tile([P, 2, CH], F32, name="acc_a", tag="acc_a", bufs=6)
-                for nn in range(2):
-                    n0 = P * (2 * n2 + nn)
-                    for a in range(2):
-                        nc.tensor.matmul_mx(
-                            out=acc[:, nn, :], lhsT=w4w[a][:, n0 : n0 + P].bitcast(FP8X4),
-                            lhsT_scale=w4s[:, a, n0 : n0 + P],
-                            rhs=rhs[a][0].bitcast(FP8X4), rhs_scale=rhs[a][1], start=(a == 0), stop=(a == 1),
-                        )
-                res = ring([P, 2, CH], F32, "res", 6)
-                nc.scalar.activation(res[:], acc[:], ACT.Gelu_apprx_tanh)
+                res = ring([P, 2, CH], F32, ("sq", "g")[n2], 4)
+                nc.scalar.activation(res[:], acc_y[c, n2][:], ACT.Gelu_apprx_tanh)
                 nc.sync.dma_start(
                     out[2 * P * n2 : 2 * P * (n2 + 1), CH * c : CH * (c + 1)].rearrange("(n p) j -> p n j", p=P),
                     res[:],

@@ -49,9 +49,9 @@ def tile_list_contact_wire_slots_kernel(
             return t
 
         def load_planes(src, name, eng, clear):
-            t = held([P, 2, src.shape[2]], U8, name)
+            t = ring([P, 2, src.shape[2]], U8, name, 1)
             clear.memset(t[:].bitcast(I32), 0)
-            for q in range(4):
+            for q in (0, 2, 1, 3):
                 eng.dma_start(
                     t[32 * q : 32 * q + 4, :, :].bitcast(I32),
                     src[:, 4 * q : 4 * q + 4, :].rearrange("a r c -> r a c").bitcast(I32),
@@ -75,26 +75,27 @@ def tile_list_contact_wire_slots_kernel(
             nc.sync.dma_start(pg[:], page0.rearrange("(b p t) s -> b t p s", b=2, t=PACK)[b, t])
             return pg
 
-        def load_wg(src, u, name):
-            t = held([P, 2, S], F32, name)
-            rows = src.rearrange("(q t) s -> q t s", t=PACK)[:, 2 * u : 2 * u + 2, :]
+        def load_wg(src, t0, t1, name):
+            tile = ring([P, t1 - t0, S], F32, name, 1)
+            rows = src.rearrange("(q t) s -> q t s", t=PACK)[:, t0:t1, :]
             for q in (0, 2, 1, 3):
-                nc.sync.dma_start(t[32 * q : 32 * q + 32, :, :], rows)
-            return t
+                nc.sync.dma_start(tile[32 * q : 32 * q + 32, :, :], rows)
+            return {t: tile[:, t - t0, :] for t in range(t0, t1)}
 
-        def quantize(src, width, tag, bufs, codes_in=None):
+        def quantize(src, width, tag, bufs, codes_in=None, scales=None):
             codes = ring([P, width], U32, codes_in or tag + "_codes", 1 if codes_in else bufs)
-            scales = ring([P, width], U8, tag + "_scales", bufs)
-            nc.vector.quantize_mx(out=codes[:].bitcast(FP8X4), scales=scales[:], in_=src)
+            if scales is None:
+                scales = ring([P, width], U8, tag + "_scales", bufs)[:]
+            nc.vector.quantize_mx(out=codes[:].bitcast(FP8X4), scales=scales, in_=src)
             return codes, scales
 
-        def quantize_w(raw, tag):
+        def quantize_w(raw, tag, scales=None, copy=nc.scalar.copy):
             wb = ring([P, PACK * KP], BF16, "grouped", 4)
-            nc.scalar.copy(
+            copy(
                 wb[:].rearrange("p (t m j) -> p m j t", t=PACK, j=PACK),
                 raw[:].rearrange("p j (m t) -> p m j t", t=PACK),
             )
-            return quantize(wb[:], KP, tag, 4)
+            return quantize(wb[:], KP, tag, 4, None, scales)
 
         def interleave(eng_copy, planes, c0, width, g=None):
             if g is None:
@@ -105,43 +106,42 @@ def tile_list_contact_wire_slots_kernel(
             )
             return g
 
-        warm = held([P, 2], F32, "warm")
-        nc.gpsimd.memset(warm[:, 0:1], 0.0)
-        nc.scalar.activation(warm[:, 1:2], warm[:, 0:1], ACT.Gelu_apprx_tanh)
         tab2w, tabw, w1raw, w3raw, pages = {}, {}, {}, {}, {}
         o2 = load_list(offs2, "o2")
         tab2w[0] = load_words(tab2_words[0], "k4", 3)
         w2raw = ring([P, 2, 2 * H], U8, "k4", 3)
         nc.sync.dma_start(w2raw[:].bitcast(I32), w2_words.rearrange("a p c -> p a c").bitcast(I32))
         tab2w[1] = load_words(tab2_words[1], "k4", 3)
-        w1raw[0, 0] = load_w(w1, 0, 0, "s0")
-        tab2s = load_planes(tab2_scales, "tab2s", nc.sync, nc.gpsimd)
-        w1raw[1, 0] = load_w(w1, 1, 0, "s1")
-        w2sraw = load_planes(w2_scales, "w2sraw", nc.sync, nc.vector)
-        fgt = load_vec(fg, "fgt")
         o1 = load_list(offs, "o1")
+        tab2s = load_planes(tab2_scales, "tab2s", nc.sync, nc.gpsimd)
+        w1raw[0, 0] = load_w(w1, 0, 0, "s0")
+        w2sraw = load_planes(w2_scales, "w2sraw", nc.sync, nc.vector)
+        w1raw[1, 0] = load_w(w1, 1, 0, "s1")
+        fgt = load_vec(fg, "fgt")
         tabw[0] = load_words(tab_words[0], "s2", 1)
-        tabs = held([P, T], U8, "tabs")
+        warm = held([P, 2], F32, "warm")
+        nc.gpsimd.memset(warm[:, 0:1], 0.0)
+        nc.scalar.activation(warm[:, 1:2], warm[:, 0:1], ACT.Gelu_apprx_tanh)
+        tabs = ring([P, T], U8, "tabs", 1)
         nc.gpsimd.memset(tabs[:].bitcast(I32), 0)
-        for q in range(4):
+        for q in (0, 2, 1, 3):
             nc.sync.dma_start(
                 tabs[32 * q : 32 * q + 8, :].bitcast(I32), tab_scales[:, 4 * q : 4 * q + 4, :].bitcast(I32)
             )
-        tabw[1] = load_words(tab_words[1], "s3", 1)
-        wg2t = {0: load_wg(wg2, 0, "wg2_0")}
-        o3 = load_list(offs3, "o3")
         sgt = load_vec(sg, "sgt")
-        wg1t = {0: load_wg(wg1, 0, "wg1_0")}
+        tabw[1] = load_words(tab_words[1], "s3", 1)
+        wg2t = load_wg(wg2, 0, 2, "wg2_0")
         pages[0, 0] = load_page(0, 0, "s4")
+        o3 = load_list(offs3, "o3")
+        wg1t = load_wg(wg1, 0, 1, "wg1_0")
         w3raw[0, 0] = load_w(w3, 0, 0, "s5")
         w3raw[1, 0] = load_w(w3, 1, 0, "s7")
+        wg1t = {**wg1t, **load_wg(wg1, 1, 2, "wg1_1")}
         pages[0, 1] = load_page(0, 1, "s6")
         o4 = load_list(offs4, "o4")
         o5 = load_list(offs5, "o5")
         pvt = load_vec(pv, "pvt")
-        wg1t[1] = load_wg(wg1, 1, "wg1_1")
         w1raw[0, 1] = load_w(w1, 0, 1, "s9")
-        wg2t[1] = load_wg(wg2, 1, "wg2_1")
         w1raw[1, 1] = load_w(w1, 1, 1, "s8")
         w4s = load_planes(w4_scales, "w4s", nc.sync, nc.gpsimd)
 
@@ -161,7 +161,8 @@ def tile_list_contact_wire_slots_kernel(
             w2sraw[:].rearrange("p a (b q t) -> p (a b) t q", b=2, t=PACK),
         )
 
-        w1q = {(a, 0): quantize_w(w1raw[a, 0], "w1") for a in range(2)}
+        w1s0 = ring([P, 2, KP], U8, "w2sraw", 1)
+        w1q = {(a, 0): quantize_w(w1raw[a, 0], "w1", w1s0[:, a, :], (nc.scalar.copy, nc.vector.tensor_copy)[a]) for a in range(2)}
         v = [held([P, S], U32, "v_%d" % a) for a in range(2)]
         vs = held([P, S], U8, "vs")
         nc.vector.tensor_copy(vs[:], tabs[:].indirect(o1[:]))
@@ -169,8 +170,10 @@ def tile_list_contact_wire_slots_kernel(
             nc.vector.tensor_copy(v[a][:], tabw[a][:].bitcast(U32).indirect(o1[:]))
 
         w3raw[0, 1] = load_w(w3, 0, 1, "s0")
+        wg2t = {**wg2t, **load_wg(wg2, 2, 4, "tab2s")}
         w3raw[1, 1] = load_w(w3, 1, 1, "s1")
         pages[0, 2] = load_page(0, 2, "s2")
+        wg1t = {**wg1t, **load_wg(wg1, 2, 4, "tabs")}
 
         h1 = {}
         sq1 = []
@@ -184,20 +187,19 @@ def tile_list_contact_wire_slots_kernel(
                     lhsT_scale=scales[:, P * t : P * (t + 1)],
                     rhs=v[a][:].bitcast(FP8X4), rhs_scale=vs[4 * a : P, :], start=(a == 0), stop=(a == 1),
                 )
-            sq = ring([P, S], F32, "sq", 4)[:] if b == 0 else sq1[0][:, t, :]
+            sq = ring([P, S], F32, "sq" if t else "sq00", 4 if t else 1)[:] if b == 0 else sq1[0][:, t, :]
             nc.scalar.activation(sq, acc[:], ACT.Square)
             nc.scalar.activation(sq, sq, ACT.Copy, scale=sgt[:, b, t : t + 1])
             h1[b, t] = sq
 
         def put_h1(b, t):
-            nc.vector.tensor_tensor(pages[b, t][:].indirect(o3[:]), h1[b, t], wg1t[t // 2][:, t % 2, :], MULT)
+            nc.vector.tensor_tensor(pages[b, t][:].indirect(o3[:]), h1[b, t], wg1t[t], MULT)
 
         make_h1(0, 0)
         put_h1(0, 0)
 
         fw = {}
         tfq = []
-        tfg = ring([P, 2, PACK * S], BF16, "s3", 1)
         tfp = ring([P, 2, PACK, S], BF16, "planes", 1)
         for b in range(2):
             for t in range(PACK):
@@ -212,9 +214,9 @@ def tile_list_contact_wire_slots_kernel(
                 th = ring([P, S], F32, "th", 2)
                 nc.scalar.activation(th[:], acc[:], ACT.Tanh)
                 fw[b, t] = ring([P, S], F32, "fw_%d_%d" % (b, t), 1)
-                nc.vector.tensor_tensor(fw[b, t][:], acc[:], wg2t[t // 2][:, t % 2, :], MULT)
+                nc.vector.tensor_tensor(fw[b, t][:], acc[:], wg2t[t], MULT)
                 nc.scalar.activation(tfp[:, b, t, :], th[:], ACT.Copy, scale=fgt[:, b, t : t + 1])
-            tfq.append(quantize(interleave(nc.vector.tensor_copy, tfp[:, b], 0, S, tfg[:, b, :]), S, "tf", 2))
+            tfq.append(quantize(interleave(nc.vector.tensor_copy, tfp[:, b], 0, S, ring([P, PACK * S], BF16, ("s3", "sq00")[b], 1)[:]), S, "tf", 2))
             if b == 0:
                 make_h1(0, 1)
                 put_h1(0, 1)
@@ -230,7 +232,7 @@ def tile_list_contact_wire_slots_kernel(
                 nc.tensor.matmul_mx(
                     out=acc[:], lhsT=codes[:, P * t : P * (t + 1)].bitcast(FP8X4),
                     lhsT_scale=scales[:, P * t : P * (t + 1)],
-                    rhs=tfq[a][0][:].bitcast(FP8X4), rhs_scale=tfq[a][1][:], start=(a == 0), stop=(a == 1),
+                    rhs=tfq[a][0][:].bitcast(FP8X4), rhs_scale=tfq[a][1], start=(a == 0), stop=(a == 1),
                 )
             g[b, t] = ring([P, S], F32, "g", 4)
             nc.scalar.copy(g[b, t][:], acc[:])
@@ -309,7 +311,7 @@ def tile_list_contact_wire_slots_kernel(
                 )
         for c in range(PJ // CH):
             codes, scales = quantize(interleave(nc.vector.tensor_copy, xp1, CH * c, CH), CH, "x1", 4)
-            y_pass(1, c, codes[:], scales[:])
+            y_pass(1, c, codes[:], scales)
             for n2 in range(2):
                 res = ring([P, 2, CH], F32, ("sq", "g")[n2], 4)
                 nc.scalar.activation(res[:], acc_y[c, n2][:], ACT.Gelu_apprx_tanh)

@@ -89,9 +89,9 @@ def tile_list_contact_wire_slots_kernel(
             nc.vector.quantize_mx(out=codes[:].bitcast(FP8X4), scales=scales, in_=src)
             return codes, scales
 
-        def quantize_w(raw, tag, scales=None, copy=nc.scalar.copy):
+        def quantize_w(raw, tag, scales=None):
             wb = ring([P, PACK * KP], BF16, "grouped", 4)
-            copy(
+            nc.scalar.copy(
                 wb[:].rearrange("p (t m j) -> p m j t", t=PACK, j=PACK),
                 raw[:].rearrange("p j (m t) -> p m j t", t=PACK),
             )
@@ -112,12 +112,12 @@ def tile_list_contact_wire_slots_kernel(
         w2raw = ring([P, 2, 2 * H], U8, "k4", 3)
         nc.sync.dma_start(w2raw[:].bitcast(I32), w2_words.rearrange("a p c -> p a c").bitcast(I32))
         tab2w[1] = load_words(tab2_words[1], "k4", 3)
-        o1 = load_list(offs, "o1")
-        tab2s = load_planes(tab2_scales, "tab2s", nc.sync, nc.gpsimd)
         w1raw[0, 0] = load_w(w1, 0, 0, "s0")
-        w2sraw = load_planes(w2_scales, "w2sraw", nc.sync, nc.vector)
+        tab2s = load_planes(tab2_scales, "tab2s", nc.sync, nc.gpsimd)
         w1raw[1, 0] = load_w(w1, 1, 0, "s1")
+        w2sraw = load_planes(w2_scales, "w2sraw", nc.sync, nc.vector)
         fgt = load_vec(fg, "fgt")
+        o1 = load_list(offs, "o1")
         tabw[0] = load_words(tab_words[0], "s2", 1)
         warm = held([P, 2], F32, "warm")
         nc.gpsimd.memset(warm[:, 0:1], 0.0)
@@ -141,9 +141,10 @@ def tile_list_contact_wire_slots_kernel(
         o4 = load_list(offs4, "o4")
         o5 = load_list(offs5, "o5")
         pvt = load_vec(pv, "pvt")
+        wg2t = {**wg2t, **load_wg(wg2, 2, 4, "wg2_2")}
+        pages[0, 2] = load_page(0, 2, "s8")
+        wg1t = {**wg1t, **load_wg(wg1, 2, 4, "wg1_2")}
         w1raw[0, 1] = load_w(w1, 0, 1, "s9")
-        w1raw[1, 1] = load_w(w1, 1, 1, "s8")
-        w4s = load_planes(w4_scales, "w4s", nc.sync, nc.gpsimd)
 
         v2 = [ring([P, S], U32, "v2", 2) for a in range(2)]
         v2s = [held([P, S], U8, "v2s_%d" % a) for a in range(2)]
@@ -162,18 +163,16 @@ def tile_list_contact_wire_slots_kernel(
         )
 
         w1s0 = ring([P, 2, KP], U8, "w2sraw", 1)
-        w1q = {(a, 0): quantize_w(w1raw[a, 0], "w1", w1s0[:, a, :], (nc.scalar.copy, nc.vector.tensor_copy)[a]) for a in range(2)}
+        w1q = {(a, 0): quantize_w(w1raw[a, 0], "w1", w1s0[:, a, :]) for a in range(2)}
         v = [held([P, S], U32, "v_%d" % a) for a in range(2)]
         vs = held([P, S], U8, "vs")
         nc.vector.tensor_copy(vs[:], tabs[:].indirect(o1[:]))
         for a in range(2):
             nc.vector.tensor_copy(v[a][:], tabw[a][:].bitcast(U32).indirect(o1[:]))
 
-        w3raw[0, 1] = load_w(w3, 0, 1, "s0")
-        wg2t = {**wg2t, **load_wg(wg2, 2, 4, "tab2s")}
-        w3raw[1, 1] = load_w(w3, 1, 1, "s1")
-        pages[0, 2] = load_page(0, 2, "s2")
-        wg1t = {**wg1t, **load_wg(wg1, 2, 4, "tabs")}
+        w1raw[1, 1] = load_w(w1, 1, 1, "s0")
+        pages[0, 3] = load_page(0, 3, "s1")
+        w3raw[0, 1] = load_w(w3, 0, 1, "s2")
 
         h1 = {}
         sq1 = []
@@ -221,7 +220,8 @@ def tile_list_contact_wire_slots_kernel(
                 make_h1(0, 1)
                 put_h1(0, 1)
 
-        pages[0, 3] = load_page(0, 3, "s3")
+        w3raw[1, 1] = load_w(w3, 1, 1, "s3")
+        w4s = load_planes(w4_scales, "tabs", nc.sync, nc.gpsimd)
         w4w = [load_words(w4_words[a], "v2", 2) for a in range(2)]
         g = {}
 
@@ -250,10 +250,10 @@ def tile_list_contact_wire_slots_kernel(
         for a in range(2):
             w1q[a, 1] = quantize_w(w1raw[a, 1], "w1")
         pages[1, 2] = load_page(1, 2, "s9")
-        pages[1, 3] = load_page(1, 3, "s8")
+        pages[1, 3] = load_page(1, 3, "s0")
         for a in range(2):
             w3q[a, 1] = quantize_w(w3raw[a, 1], "w3")
-        sq1.append(ring([P, PACK, S], F32, "s1", 1))
+        sq1.append(ring([P, PACK, S], F32, "s3", 1))
         for t in range(PACK):
             make_h1(1, t)
 
@@ -262,7 +262,7 @@ def tile_list_contact_wire_slots_kernel(
             nc.vector.tensor_copy(xg[:], pages[b, t][:].indirect(o5[:, c0 // 16 : (c0 + width) // 16]))
             nc.scalar.activation(planes[:, t, c0 : c0 + width], xg[:], ACT.Identity, bias=pvt[:, b, t : t + 1])
 
-        xp0 = ring([P, PACK, PJ], BF16, "s0", 1)
+        xp0 = ring([P, PACK, PJ], BF16, "s2", 1)
         for t in range(PACK):
             if t >= 2:
                 put_h1(0, t)
@@ -271,7 +271,7 @@ def tile_list_contact_wire_slots_kernel(
             fetch(0, t, xp0, 0, PJ, "k4", 3)
 
         x0g = [interleave(nc.scalar.copy, xp0, S * h, S) for h in range(2)]
-        xp1 = ring([P, PACK, PJ], BF16, "s0", 1)
+        xp1 = ring([P, PACK, PJ], BF16, "s2", 1)
         acc_y = {}
 
         def y_pass(a, c, codes, scales):

@@ -1,9 +1,11 @@
 from contextlib import ExitStack
 
 import concourse.mybir as mybir
+from concourse.masks import make_identity
 
-K, H, N, T, TB, S, T2, PJ = 1024, 1024, 512, 2048, 1024, 512, 2048, 1024
-FLOPS = 2 * (K * H * S * 2 + H * H * S + H * N * PJ)
+K, H, N = 1024, 1024, 512
+S, T2, PJ = 512, 2048, 1024
+FLOPS = 2 * (2 * K * H * S + H * H * S + H * N * PJ)
 
 F32 = mybir.dt.float32
 BF16 = mybir.dt.bfloat16
@@ -19,7 +21,12 @@ MULT = mybir.AluOpType.mult
 P = 128
 PACK = 4
 KP = P * PACK
+PASSES = 2
+QUAD = 32
+QUADRANTS = (0, 2, 1, 3)
+LIST_ROWS = 16
 CH = 256
+F_BANKS, STEP_BANKS = 6, 2
 
 
 def tile_list_contact_wire_slots_kernel(
@@ -35,287 +42,328 @@ def tile_list_contact_wire_slots_kernel(
         def held(shape, dtype, name):
             return keep.tile(shape, dtype, name=name, align_bytes=64)
 
-        def ring(shape, dtype, tag, bufs):
+        def shared(shape, dtype, tag, bufs=1):
             return work.tile(shape, dtype, name=tag, tag=tag, bufs=bufs, align_bytes=64)
 
+        def f_bank(shape):
+            return psum.tile(shape, F32, name="f_bank", tag="f_bank", bufs=F_BANKS)
+
+        def step_bank(shape):
+            return psum.tile(shape, F32, name="step_bank", tag="step_bank", bufs=STEP_BANKS)
+
+        def staged(shape, dtype):
+            return shared(shape, dtype, "staged", 3)
+
+        def grouped(width):
+            return shared([P, PACK * width], BF16, "grouped", 4)[:]
+
         def load_list(src, name):
-            t = keep.tile(list(src.shape), U16, name=name)
-            nc.sync.dma_start(t[:], src)
-            return t
+            tile = keep.tile(list(src.shape), U16, name=name)
+            nc.sync.dma_start(tile[:], src)
+            return tile
 
-        def load_words(src, tag, bufs):
-            t = ring([P, src.shape[1]], I32, tag, bufs)
-            nc.sync.dma_start(t[:], src.rearrange("p t i -> p (t i)").bitcast(I32))
-            return t
+        def load_words(tile, src):
+            nc.sync.dma_start(tile[:], src.rearrange("p c i -> p (c i)").bitcast(I32))
+            return tile
 
-        def load_planes(src, name, eng, clear):
-            t = ring([P, 2, src.shape[2]], U8, name, 1)
-            clear.memset(t[:].bitcast(I32), 0)
-            for q in (0, 2, 1, 3):
-                eng.dma_start(
-                    t[32 * q : 32 * q + 4, :, :].bitcast(I32),
+        def load_scales(src, tag, clear):
+            tile = shared([P, PASSES, src.shape[2]], U8, tag)
+            clear.memset(tile[:].bitcast(I32), 0)
+            for q in QUADRANTS:
+                nc.sync.dma_start(
+                    tile[QUAD * q : QUAD * q + 4, :, :].bitcast(I32),
                     src[:, 4 * q : 4 * q + 4, :].rearrange("a r c -> r a c").bitcast(I32),
                 )
-            return t
+            return tile
 
-        def load_vec(src, name):
-            t = held([P, 2, PACK], F32, name)
-            nc.sync.dma_start(t[:], src.rearrange("(b p t) -> p b t", b=2, t=PACK))
-            return t
+        def load_channels(src, name):
+            tile = held([P, PASSES, PACK], F32, name)
+            nc.sync.dma_start(tile[:], src.rearrange("(b p t) -> p b t", b=PASSES, t=PACK))
+            return tile
 
-        def load_w(src, a, b, tag):
-            t = ring([P, PACK, KP], F32, tag, 1)
+        def load_weight(src, a, b, tag):
+            tile = shared([P, PACK, KP], F32, tag)
             nc.sync.dma_start(
-                t[:], src[KP * a : KP * (a + 1), KP * b : KP * (b + 1)].rearrange("(p j) c -> p j c", j=PACK)
+                tile[:], src[KP * a : KP * (a + 1), KP * b : KP * (b + 1)].rearrange("(p j) c -> p j c", j=PACK)
             )
-            return t
+            return tile
 
         def load_page(b, t, tag):
-            pg = ring([P, T2], F32, tag, 1)
-            nc.sync.dma_start(pg[:], page0.rearrange("(b p t) s -> b t p s", b=2, t=PACK)[b, t])
-            return pg
+            tile = shared([P, T2], F32, tag)
+            nc.sync.dma_start(tile[:], page0.rearrange("(b p t) s -> b t p s", b=PASSES, t=PACK)[b, t])
+            return tile
 
-        def load_wg(src, t0, t1, name):
-            tile = ring([P, t1 - t0, S], F32, name, 1)
-            rows = src.rearrange("(q t) s -> q t s", t=PACK)[:, t0:t1, :]
-            for q in (0, 2, 1, 3):
-                nc.sync.dma_start(tile[32 * q : 32 * q + 32, :, :], rows)
-            return {t: tile[:, t - t0, :] for t in range(t0, t1)}
+        def load_wg1(t0, t1, tag):
+            tile = shared([P, t1 - t0, S], F32, tag)
+            rows = wg1.rearrange("(q t) s -> q t s", t=PACK)[:, t0:t1, :]
+            for q in QUADRANTS:
+                nc.sync.dma_start(tile[QUAD * q : QUAD * (q + 1), :, :], rows)
+            return [tile[:, t - t0, :] for t in range(t0, t1)]
 
-        def quantize(src, width, tag, bufs, codes_in=None, scales=None):
-            codes = ring([P, width], U32, codes_in or tag + "_codes", 1 if codes_in else bufs)
-            if scales is None:
-                scales = ring([P, width], U8, tag + "_scales", bufs)[:]
-            nc.vector.quantize_mx(out=codes[:].bitcast(FP8X4), scales=scales, in_=src)
+        def quantize(src, codes, scales):
+            nc.vector.quantize_mx(out=codes.bitcast(FP8X4), scales=scales, in_=src)
             return codes, scales
 
-        def quantize_w(raw, tag, scales=None):
-            wb = ring([P, PACK * KP], BF16, "grouped", 4)
+        def mx_tiles(width, tag, bufs):
+            return shared([P, width], U32, tag + "_codes", bufs)[:], shared([P, width], U8, tag + "_scales", bufs)[:]
+
+        def round_weight(raw):
+            dst = grouped(KP)
             nc.scalar.copy(
-                wb[:].rearrange("p (t m j) -> p m j t", t=PACK, j=PACK),
+                dst.rearrange("p (t m j) -> p m j t", t=PACK, j=PACK),
                 raw[:].rearrange("p j (m t) -> p m j t", t=PACK),
             )
-            return quantize(wb[:], KP, tag, 4, None, scales)
+            return dst
 
-        def interleave(eng_copy, planes, c0, width, g=None):
-            if g is None:
-                g = ring([P, PACK * width], BF16, "grouped", 4)[:]
-            eng_copy(
-                g.rearrange("p (c i t) -> p c t i", i=4, t=PACK),
-                planes[:, :, c0 : c0 + width].rearrange("p t (c i) -> p c t i", i=4),
+        def interleave(copy, dst, slices):
+            copy(
+                dst.rearrange("p (c i t) -> p c t i", i=4, t=PACK),
+                slices.rearrange("p t (c i) -> p c t i", i=4),
             )
-            return g
+            return dst
 
-        tab2w, tabw, w1raw, w3raw, pages = {}, {}, {}, {}, {}
-        o2 = load_list(offs2, "o2")
-        tab2w[0] = load_words(tab2_words[0], "k4", 3)
-        w2raw = ring([P, 2, 2 * H], U8, "k4", 3)
-        nc.sync.dma_start(w2raw[:].bitcast(I32), w2_words.rearrange("a p c -> p a c").bitcast(I32))
-        tab2w[1] = load_words(tab2_words[1], "k4", 3)
-        w1raw[0, 0] = load_w(w1, 0, 0, "s0")
-        tab2s = load_planes(tab2_scales, "tab2s", nc.sync, nc.gpsimd)
-        w1raw[1, 0] = load_w(w1, 1, 0, "s1")
-        w2sraw = load_planes(w2_scales, "w2sraw", nc.sync, nc.vector)
-        fgt = load_vec(fg, "fgt")
-        o1 = load_list(offs, "o1")
-        tabw[0] = load_words(tab_words[0], "s2", 1)
-        warm = held([P, 2], F32, "warm")
-        nc.gpsimd.memset(warm[:, 0:1], 0.0)
-        nc.scalar.activation(warm[:, 1:2], warm[:, 0:1], ACT.Gelu_apprx_tanh)
-        tabs = ring([P, T], U8, "tabs", 1)
-        nc.gpsimd.memset(tabs[:].bitcast(I32), 0)
-        for q in (0, 2, 1, 3):
+        def product(acc, stationary, moving):
+            for a in range(PASSES):
+                nc.tensor.matmul_mx(
+                    out=acc, lhsT=stationary[a][0], lhsT_scale=stationary[a][1], rhs=moving[a][0],
+                    rhs_scale=moving[a][1], start=(a == 0), stop=(a == PASSES - 1),
+                )
+
+        def columns(weight, b, t):
+            cols = slice(P * t, P * (t + 1))
+            return [(weight[a, b][0][:, cols].bitcast(FP8X4), weight[a, b][1][:, cols]) for a in range(PASSES)]
+
+        tab2_w, tab_w, w1_raw, w3_raw, page = {}, {}, {}, {}, {}
+        idx2 = load_list(offs2, "idx2")
+        wg2_rows = shared([P, S], F32, "tanh", 2)
+        nc.sync.dma_start(wg2_rows[:], wg2)
+        tab2_w[0] = load_words(staged([P, tab2_words.shape[2]], I32), tab2_words[0])
+        w2_raw = staged([P, PASSES, 2 * H], U8)
+        nc.sync.dma_start(w2_raw[:].bitcast(I32), w2_words.rearrange("a p c -> p a c").bitcast(I32))
+        tab2_w[1] = load_words(staged([P, tab2_words.shape[2]], I32), tab2_words[1])
+        tab2_s = load_scales(tab2_scales, "tab2_s", nc.gpsimd)
+        w1_raw[0, 0] = load_weight(w1, 0, 0, "big0")
+        w2_raw_s = load_scales(w2_scales, "w2_raw_s", nc.vector)
+        w1_raw[1, 0] = load_weight(w1, 1, 0, "big1")
+        fg_t = load_channels(fg, "fg_t")
+        idx1 = load_list(offs, "idx1")
+        zero = held([P, 2], F32, "zero")
+        nc.gpsimd.memset(zero[:, 0:1], 0.0)
+        nc.scalar.activation(zero[:, 1:2], zero[:, 0:1], ACT.Gelu_apprx_tanh)
+        tab_s = shared([P, tab_scales.shape[2]], U8, "tab_s")
+        nc.gpsimd.memset(tab_s[:].bitcast(I32), 0)
+        for q in QUADRANTS:
             nc.sync.dma_start(
-                tabs[32 * q : 32 * q + 8, :].bitcast(I32), tab_scales[:, 4 * q : 4 * q + 4, :].bitcast(I32)
+                tab_s[QUAD * q : QUAD * q + 4 * PASSES, :].bitcast(I32), tab_scales[:, 4 * q : 4 * q + 4, :].bitcast(I32)
             )
-        sgt = load_vec(sg, "sgt")
-        tabw[1] = load_words(tab_words[1], "s3", 1)
-        wg2t = load_wg(wg2, 0, 2, "wg2_0")
-        pages[0, 0] = load_page(0, 0, "s4")
-        o3 = load_list(offs3, "o3")
-        wg1t = load_wg(wg1, 0, 1, "wg1_0")
-        w3raw[0, 0] = load_w(w3, 0, 0, "s5")
-        w3raw[1, 0] = load_w(w3, 1, 0, "s7")
-        wg1t = {**wg1t, **load_wg(wg1, 1, 2, "wg1_1")}
-        pages[0, 1] = load_page(0, 1, "s6")
-        o4 = load_list(offs4, "o4")
-        o5 = load_list(offs5, "o5")
-        pvt = load_vec(pv, "pvt")
-        wg2t = {**wg2t, **load_wg(wg2, 2, 4, "wg2_2")}
-        pages[0, 2] = load_page(0, 2, "s8")
-        wg1t = {**wg1t, **load_wg(wg1, 2, 4, "wg1_2")}
-        w1raw[0, 1] = load_w(w1, 0, 1, "s9")
+        tab_w[0] = load_words(shared([P, tab_words.shape[2]], I32, "big2"), tab_words[0])
+        sg_t = load_channels(sg, "sg_t")
+        tab_w[1] = load_words(shared([P, tab_words.shape[2]], I32, "big3"), tab_words[1])
+        page[0, 0] = load_page(0, 0, "big4")
+        idx3 = load_list(offs3, "idx3")
+        wg1_t = load_wg1(0, 1, "wg1_0")
+        w3_raw[0, 0] = load_weight(w3, 0, 0, "big5")
+        w3_raw[1, 0] = load_weight(w3, 1, 0, "big7")
+        wg1_t = wg1_t + load_wg1(1, 2, "wg1_1")
+        page[0, 1] = load_page(0, 1, "big6")
+        idx4 = load_list(offs4, "idx4")
+        idx5 = load_list(offs5, "idx5")
+        pv_t = load_channels(pv, "pv_t")
+        page[0, 2] = load_page(0, 2, "big8")
+        wg1_t = wg1_t + load_wg1(2, PACK, "wg1_23")
+        w1_raw[0, 1] = load_weight(w1, 0, 1, "big9")
 
-        v2 = [ring([P, S], U32, "v2", 2) for a in range(2)]
-        v2s = [held([P, S], U8, "v2s_%d" % a) for a in range(2)]
-        w2p = [held([P, 2 * H], U8, "w2p_%d" % a) for a in range(2)]
-        w2sp = held([P, 2, H], U8, "w2sp")
-        for a in range(2):
-            nc.vector.tensor_copy(v2[a][:], tab2w[a][:].bitcast(U32).indirect(o2[:]))
+        ident = held([P, P], F32, "ident")
+        make_identity(nc, ident[:])
+        blocks = S // P
+        turned = f_bank([P, blocks, P])
+        for jb in range(blocks):
+            nc.tensor.transpose(turned[:, jb, :], wg2_rows[:, P * jb : P * (jb + 1)], ident[:])
+        spread = shared([P, blocks, PACK, P // QUAD, QUAD], F32, "slices")
+        nc.scalar.copy(
+            spread[:],
+            turned[:].rearrange("p b (q t) -> p b t q", t=PACK).unsqueeze(3).to_broadcast(list(spread[:].shape)),
+        )
+        wg2_t = held([P, PACK, S], F32, "wg2_t")
+        for t in range(PACK):
+            back = f_bank([P, blocks, P])
+            for jb in range(blocks):
+                nc.tensor.transpose(back[:, jb, :], spread[:, jb, t].rearrange("p g q -> p (g q)"), ident[:])
+            nc.scalar.copy(wg2_t[:, t, :], back[:].rearrange("p b j -> p (b j)"))
+
+        v2 = [shared([P, S], U32, "v2", PASSES) for a in range(PASSES)]
+        v2_s = [held([P, S], U8, "v2_s%d" % a) for a in range(PASSES)]
+        w2_w = [held([P, 2 * H], U8, "w2_w%d" % a) for a in range(PASSES)]
+        w2_s = held([P, PASSES, H], U8, "w2_s")
+        for a in range(PASSES):
+            nc.vector.tensor_copy(v2[a][:], tab2_w[a][:].bitcast(U32).indirect(idx2[:]))
             nc.vector.tensor_copy(
-                w2p[a][:].bitcast(U16).rearrange("p (b t q) -> p b t q", b=2, t=PACK),
-                w2raw[:, a, :].bitcast(U16).rearrange("p (b q t) -> p b t q", b=2, t=PACK),
+                w2_w[a][:].bitcast(U16).rearrange("p (b t q) -> p b t q", b=PASSES, t=PACK),
+                w2_raw[:, a, :].bitcast(U16).rearrange("p (b q t) -> p b t q", b=PASSES, t=PACK),
             )
-            nc.vector.tensor_copy(v2s[a][:], tab2s[:, a, :].indirect(o2[:]))
+            nc.vector.tensor_copy(v2_s[a][:], tab2_s[:, a, :].indirect(idx2[:]))
         nc.vector.tensor_copy(
-            w2sp[:].rearrange("p a (b t q) -> p (a b) t q", b=2, t=PACK),
-            w2sraw[:].rearrange("p a (b q t) -> p (a b) t q", b=2, t=PACK),
+            w2_s[:].rearrange("p a (b t q) -> p (a b) t q", b=PASSES, t=PACK),
+            w2_raw_s[:].rearrange("p a (b q t) -> p (a b) t q", b=PASSES, t=PACK),
         )
 
-        w1s0 = ring([P, 2, KP], U8, "w2sraw", 1)
-        w1q = {(a, 0): quantize_w(w1raw[a, 0], "w1", w1s0[:, a, :]) for a in range(2)}
-        v = [held([P, S], U32, "v_%d" % a) for a in range(2)]
-        vs = held([P, S], U8, "vs")
-        nc.vector.tensor_copy(vs[:], tabs[:].indirect(o1[:]))
-        for a in range(2):
-            nc.vector.tensor_copy(v[a][:], tabw[a][:].bitcast(U32).indirect(o1[:]))
+        w1_s0 = shared([P, PASSES, KP], U8, "w2_raw_s")
+        w1_q = {}
+        for a in range(PASSES):
+            w1_q[a, 0] = quantize(round_weight(w1_raw[a, 0]), shared([P, KP], U32, "w1_codes", 4)[:], w1_s0[:, a, :])
+        v = [held([P, S], U32, "v%d" % a) for a in range(PASSES)]
+        v_s = held([P, S], U8, "v_s")
+        nc.vector.tensor_copy(v_s[:], tab_s[:].indirect(idx1[:]))
+        for a in range(PASSES):
+            nc.vector.tensor_copy(v[a][:], tab_w[a][:].bitcast(U32).indirect(idx1[:]))
+        v_mx = [(v[a][:].bitcast(FP8X4), v_s[4 * a : P, :]) for a in range(PASSES)]
 
-        w1raw[1, 1] = load_w(w1, 1, 1, "s0")
-        pages[0, 3] = load_page(0, 3, "s1")
-        w3raw[0, 1] = load_w(w3, 0, 1, "s2")
+        w1_raw[1, 1] = load_weight(w1, 1, 1, "big0")
+        page[0, 3] = load_page(0, 3, "big1")
+        w3_raw[0, 1] = load_weight(w3, 0, 1, "big2")
 
         h1 = {}
-        sq1 = []
 
-        def make_h1(b, t):
-            acc = psum.tile([P, S], F32, name="acc_b", tag="acc_b", bufs=2)
-            for a in range(2):
-                codes, scales = w1q[a, b]
-                nc.tensor.matmul_mx(
-                    out=acc[:], lhsT=codes[:, P * t : P * (t + 1)].bitcast(FP8X4),
-                    lhsT_scale=scales[:, P * t : P * (t + 1)],
-                    rhs=v[a][:].bitcast(FP8X4), rhs_scale=vs[4 * a : P, :], start=(a == 0), stop=(a == 1),
-                )
-            sq = ring([P, S], F32, "sq" if t else "sq00", 4 if t else 1)[:] if b == 0 else sq1[0][:, t, :]
-            nc.scalar.activation(sq, acc[:], ACT.Square)
-            nc.scalar.activation(sq, sq, ACT.Copy, scale=sgt[:, b, t : t + 1])
-            h1[b, t] = sq
+        def make_h1(b, t, dst):
+            acc = step_bank([P, S])
+            product(acc[:], columns(w1_q, b, t), v_mx)
+            nc.scalar.activation(dst, acc[:], ACT.Square)
+            nc.scalar.activation(dst, dst, ACT.Copy, scale=sg_t[:, b, t : t + 1])
+            h1[b, t] = dst
 
         def put_h1(b, t):
-            nc.vector.tensor_tensor(pages[b, t][:].indirect(o3[:]), h1[b, t], wg1t[t], MULT)
+            nc.vector.tensor_tensor(page[b, t][:].indirect(idx3[:]), h1[b, t], wg1_t[t], MULT)
 
-        make_h1(0, 0)
+        def h1_tile():
+            return shared([P, S], F32, "h1", PACK)[:]
+
+        make_h1(0, 0, shared([P, S], F32, "first_h1")[:])
         put_h1(0, 0)
 
+        after_first = shared([P, 3 * S], F32, "first_h1")
+        tf_slices = shared([P, PASSES, PACK, S], BF16, "slices")
+        v2_mx = [(v2[a][:].bitcast(FP8X4), v2_s[a][:]) for a in range(PASSES)]
         fw = {}
-        tfq = []
-        tfp = ring([P, 2, PACK, S], BF16, "planes", 1)
-        for b in range(2):
+        tf_mx = []
+        for b in range(PASSES):
             for t in range(PACK):
-                acc = psum.tile([P, S], F32, name="acc_a", tag="acc_a", bufs=6)
+                acc = f_bank([P, S])
                 c0 = KP * b + P * t
-                for a in range(2):
-                    nc.tensor.matmul_mx(
-                        out=acc[:], lhsT=w2p[a][:, 2 * c0 : 2 * (c0 + P)].bitcast(FP4X4),
-                        lhsT_scale=w2sp[:, a, c0 : c0 + P],
-                        rhs=v2[a][:].bitcast(FP8X4), rhs_scale=v2s[a][:], start=(a == 0), stop=(a == 1),
-                    )
-                th = ring([P, S], F32, "th", 2)
-                nc.scalar.activation(th[:], acc[:], ACT.Tanh)
-                fw[b, t] = ring([P, S], F32, "fw_%d_%d" % (b, t), 1)
-                nc.vector.tensor_tensor(fw[b, t][:], acc[:], wg2t[t], MULT)
-                nc.scalar.activation(tfp[:, b, t, :], th[:], ACT.Copy, scale=fgt[:, b, t : t + 1])
-            tfq.append(quantize(interleave(nc.vector.tensor_copy, tfp[:, b], 0, S, ring([P, PACK * S], BF16, ("s3", "sq00")[b], 1)[:]), S, "tf", 2))
+                w2_cols = [
+                    (w2_w[a][:, 2 * c0 : 2 * (c0 + P)].bitcast(FP4X4), w2_s[:, a, c0 : c0 + P]) for a in range(PASSES)
+                ]
+                product(acc[:], w2_cols, v2_mx)
+                th = shared([P, S], F32, "tanh", 2)
+                nc.scalar.activation(th[:], acc[:], ACT.Tanh, bias=zero[:, 1:2])
+                last = (b, t) == (PASSES - 1, PACK - 1)
+                fw[b, t] = after_first[:, :S] if last else shared([P, S], F32, "fw%d%d" % (b, t))[:]
+                nc.vector.tensor_tensor(fw[b, t], acc[:], wg2_t[:, t, :], MULT)
+                nc.scalar.activation(tf_slices[:, b, t, :], th[:], ACT.Copy, scale=fg_t[:, b, t : t + 1])
+            dst = after_first[:, S:].bitcast(BF16) if b else shared([P, PACK * S], BF16, "big3")[:]
+            codes, scales = quantize(interleave(nc.vector.tensor_copy, dst, tf_slices[:, b]), *mx_tiles(S, "tf", PASSES))
+            tf_mx.append((codes.bitcast(FP8X4), scales))
             if b == 0:
-                make_h1(0, 1)
+                make_h1(0, 1, h1_tile())
                 put_h1(0, 1)
 
-        w3raw[1, 1] = load_w(w3, 1, 1, "s3")
-        w4s = load_planes(w4_scales, "tabs", nc.sync, nc.gpsimd)
-        w4w = [load_words(w4_words[a], "v2", 2) for a in range(2)]
+        w3_raw[1, 1] = load_weight(w3, 1, 1, "big3")
+        w4_s = load_scales(w4_scales, "tab_s", nc.gpsimd)
+        w4_w = [load_words(shared([P, N], I32, "v2", PASSES), w4_words[a]) for a in range(PASSES)]
+
         g = {}
 
         def make_g(b, t):
-            acc = psum.tile([P, S], F32, name="acc_b", tag="acc_b", bufs=2)
-            for a in range(2):
-                codes, scales = w3q[a, b]
-                nc.tensor.matmul_mx(
-                    out=acc[:], lhsT=codes[:, P * t : P * (t + 1)].bitcast(FP8X4),
-                    lhsT_scale=scales[:, P * t : P * (t + 1)],
-                    rhs=tfq[a][0][:].bitcast(FP8X4), rhs_scale=tfq[a][1], start=(a == 0), stop=(a == 1),
-                )
-            g[b, t] = ring([P, S], F32, "g", 4)
+            acc = step_bank([P, S])
+            product(acc[:], columns(w3_q, b, t), tf_mx)
+            g[b, t] = shared([P, S], F32, "g", PACK)
             nc.scalar.copy(g[b, t][:], acc[:])
 
         def put_h2(b, t):
-            nc.vector.tensor_tensor(pages[b, t][:].indirect(o4[:]), g[b, t][:], fw[b, t][:], MULT)
+            nc.vector.tensor_tensor(page[b, t][:].indirect(idx4[:]), g[b, t][:], fw[b, t], MULT)
 
-        w3q = {(a, 0): quantize_w(w3raw[a, 0], "w3") for a in range(2)}
-        pages[1, 0] = load_page(1, 0, "s5")
-        pages[1, 1] = load_page(1, 1, "s7")
+        w3_q = {}
+        for a in range(PASSES):
+            w3_q[a, 0] = quantize(round_weight(w3_raw[a, 0]), *mx_tiles(KP, "w3", 2 * PASSES))
+        page[1, 0] = load_page(1, 0, "big5")
+        page[1, 1] = load_page(1, 1, "big7")
         for t in range(PACK):
             make_g(0, t)
-        make_h1(0, 2)
-        make_h1(0, 3)
-        for a in range(2):
-            w1q[a, 1] = quantize_w(w1raw[a, 1], "w1")
-        pages[1, 2] = load_page(1, 2, "s9")
-        pages[1, 3] = load_page(1, 3, "s0")
-        for a in range(2):
-            w3q[a, 1] = quantize_w(w3raw[a, 1], "w3")
-        sq1.append(ring([P, PACK, S], F32, "s3", 1))
+        for t in range(2, PACK):
+            make_h1(0, t, h1_tile())
+        for a in range(PASSES):
+            w1_q[a, 1] = quantize(
+                round_weight(w1_raw[a, 1]), shared([P, KP], U32, "w1_codes", 4)[:],
+                shared([P, KP], U8, "w1_scales", PASSES)[:],
+            )
+        page[1, 2] = load_page(1, 2, "big9")
+        page[1, 3] = load_page(1, 3, "big0")
+        for a in range(PASSES):
+            w3_q[a, 1] = quantize(round_weight(w3_raw[a, 1]), *mx_tiles(KP, "w3", 2 * PASSES))
+        h1_second = shared([P, PACK, S], F32, "big3")
         for t in range(PACK):
-            make_h1(1, t)
+            make_h1(1, t, h1_second[:, t, :])
 
-        def fetch(b, t, planes, c0, width, tag, bufs):
-            xg = ring([P, width], F32, tag, bufs)
-            nc.vector.tensor_copy(xg[:], pages[b, t][:].indirect(o5[:, c0 // 16 : (c0 + width) // 16]))
-            nc.scalar.activation(planes[:, t, c0 : c0 + width], xg[:], ACT.Identity, bias=pvt[:, b, t : t + 1])
+        def fetch(b, t, c0, width):
+            picked = staged([P, width], F32)
+            nc.vector.tensor_copy(
+                picked[:], page[b, t][:].indirect(idx5[:, c0 // LIST_ROWS : (c0 + width) // LIST_ROWS])
+            )
+            return picked
 
-        xp0 = ring([P, PACK, PJ], BF16, "s2", 1)
+        def add_pv(b, t, dst, picked):
+            nc.scalar.activation(dst, picked, ACT.Identity, bias=pv_t[:, b, t : t + 1])
+
+        x_first = shared([P, PACK, PJ], BF16, "big2")
         for t in range(PACK):
             if t >= 2:
                 put_h1(0, t)
             put_h2(0, t)
             make_g(1, t)
-            fetch(0, t, xp0, 0, PJ, "k4", 3)
+            add_pv(0, t, x_first[:, t, :], fetch(0, t, 0, PJ)[:])
+        halves = PJ // S
+        x_grouped = [interleave(nc.scalar.copy, grouped(S), x_first[:, :, S * h : S * (h + 1)]) for h in range(halves)]
 
-        x0g = [interleave(nc.scalar.copy, xp0, S * h, S) for h in range(2)]
-        xp1 = ring([P, PACK, PJ], BF16, "s2", 1)
+        x_second = shared([P, PACK, PJ], BF16, "big2")
+        chunks = PJ // CH
         acc_y = {}
 
         def y_pass(a, c, codes, scales):
             for n in range(N // P):
-                n2, nn = divmod(n, 2)
+                pair, side = divmod(n, 2)
                 nc.tensor.matmul_mx(
-                    out=acc_y[c, n2][:, nn, :], lhsT=w4w[a][:, P * n : P * (n + 1)].bitcast(FP8X4),
-                    lhsT_scale=w4s[:, a, P * n : P * (n + 1)],
-                    rhs=codes.bitcast(FP8X4), rhs_scale=scales,
-                    start=(a == 0 and nn == 0), stop=(a == 1 and nn == 1),
+                    out=acc_y[c, pair][:, side, :], lhsT=w4_w[a][:, P * n : P * (n + 1)].bitcast(FP8X4),
+                    lhsT_scale=w4_s[:, a, P * n : P * (n + 1)], rhs=codes.bitcast(FP8X4), rhs_scale=scales,
+                    start=(a == 0 and side == 0), stop=(a == PASSES - 1 and side == 1),
                 )
 
         for t in range(PACK):
             put_h1(1, t)
             put_h2(1, t)
-            if t < 2:
-                codes, scales = quantize(x0g[t], S, "x0", 2, "fw_1_%d" % t)
+            if t < halves:
+                codes, scales = quantize(
+                    x_grouped[t], shared([P, S], U32, "fw1%d" % t)[:], shared([P, S], U8, "x0_scales", halves)[:]
+                )
                 for cc in range(S // CH):
                     c = (S // CH) * t + cc
-                    for n2 in range(2):
-                        last = c == PJ // CH - 1
-                        acc_y[c, n2] = psum.tile(
-                            [P, 2, CH], F32, name="acc_y", tag="acc_b" if last else "acc_a", bufs=2 if last else 6
-                        )
+                    for pair in range(2):
+                        acc_y[c, pair] = (step_bank if c == chunks - 1 else f_bank)([P, 2, CH])
                     y_pass(0, c, codes[:, CH * cc : CH * (cc + 1)], scales[:, CH * cc : CH * (cc + 1)])
             if t < PACK - 1:
-                fetch(1, t, xp1, 0, PJ, "k4", 3)
+                add_pv(1, t, x_second[:, t, :], fetch(1, t, 0, PJ)[:])
 
-        for h in range(2):
-            xg = ring([P, S], F32, "k4", 3)
-            nc.vector.tensor_copy(xg[:], pages[1, PACK - 1][:].indirect(o5[:, S * h // 16 : S * (h + 1) // 16]))
+        t = PACK - 1
+        for h in range(halves):
+            picked = fetch(1, t, S * h, S)
             for cc in range(S // CH):
                 c0 = S * h + CH * cc
-                nc.scalar.activation(
-                    xp1[:, PACK - 1, c0 : c0 + CH], xg[:, CH * cc : CH * (cc + 1)], ACT.Identity,
-                    bias=pvt[:, 1, PACK - 1 : PACK],
-                )
-        for c in range(PJ // CH):
-            codes, scales = quantize(interleave(nc.vector.tensor_copy, xp1, CH * c, CH), CH, "x1", 4)
-            y_pass(1, c, codes[:], scales)
-            for n2 in range(2):
-                res = ring([P, 2, CH], F32, ("sq", "g")[n2], 4)
-                nc.scalar.activation(res[:], acc_y[c, n2][:], ACT.Gelu_apprx_tanh)
+                add_pv(1, t, x_second[:, t, c0 : c0 + CH], picked[:, CH * cc : CH * (cc + 1)])
+        for c in range(chunks):
+            cols = slice(CH * c, CH * (c + 1))
+            words = interleave(nc.vector.tensor_copy, grouped(CH), x_second[:, :, cols])
+            y_pass(1, c, *quantize(words, *mx_tiles(CH, "x1", chunks)))
+            for pair in range(2):
+                res = shared([P, 2, CH], F32, ("h1", "g")[pair], PACK)
+                nc.scalar.activation(res[:], acc_y[c, pair][:], ACT.Gelu_apprx_tanh)
                 nc.sync.dma_start(
-                    out[2 * P * n2 : 2 * P * (n2 + 1), CH * c : CH * (c + 1)].rearrange("(n p) j -> p n j", p=P),
-                    res[:],
+                    out[2 * P * pair : 2 * P * (pair + 1), cols].rearrange("(n p) j -> p n j", p=P), res[:]
                 )

from contextlib import ExitStack

import concourse.mybir as mybir
from concourse.masks import make_identity

K, H, N = 1024, 1024, 512
S, T2, PJ = 512, 2048, 1024
FLOPS = 2 * (2 * K * H * S + H * H * S + H * N * PJ)

F32 = mybir.dt.float32
BF16 = mybir.dt.bfloat16
I32 = mybir.dt.int32
U32 = mybir.dt.uint32
U16 = mybir.dt.uint16
U8 = mybir.dt.uint8
FP8X4 = mybir.dt.float8_e4m3fn_x4
FP4X4 = mybir.dt.float4_e2m1fn_x4
ACT = mybir.ActivationFunctionType
MULT = mybir.AluOpType.mult

P = 128
PACK = 4
KP = P * PACK
PASSES = 2
QUAD = 32
QUADRANTS = (0, 2, 1, 3)
LIST_ROWS = 16
CH = 256
F_BANKS, STEP_BANKS = 6, 2


def tile_list_contact_wire_slots_kernel(
    tc, tab_words, tab_scales, tab2_words, tab2_scales, offs, offs2, offs3, offs4, offs5,
    w1, w2_words, w2_scales, w3, w4_words, w4_scales, sg, fg, pv, wg1, wg2, page0, out,
):
    nc = tc.nc
    with ExitStack() as ctx:
        keep = ctx.enter_context(tc.tile_pool(name="keep", bufs=1))
        work = ctx.enter_context(tc.tile_pool(name="work", bufs=1))
        psum = ctx.enter_context(tc.psum_pool(name="psum", bufs=1))

        def held(shape, dtype, name):
            return keep.tile(shape, dtype, name=name, align_bytes=64)

        def shared(shape, dtype, tag, bufs=1):
            return work.tile(shape, dtype, name=tag, tag=tag, bufs=bufs, align_bytes=64)

        def f_bank(shape):
            return psum.tile(shape, F32, name="f_bank", tag="f_bank", bufs=F_BANKS)

        def step_bank(shape):
            return psum.tile(shape, F32, name="step_bank", tag="step_bank", bufs=STEP_BANKS)

        def staged(shape, dtype):
            return shared(shape, dtype, "staged", 3)

        def grouped(width):
            return shared([P, PACK * width], BF16, "grouped", 4)[:]

        def load_list(src, name):
            tile = keep.tile(list(src.shape), U16, name=name)
            nc.sync.dma_start(tile[:], src)
            return tile

        def load_words(tile, src):
            nc.sync.dma_start(tile[:], src.rearrange("p c i -> p (c i)").bitcast(I32))
            return tile

        def load_scales(src, tag, clear):
            tile = shared([P, PASSES, src.shape[2]], U8, tag)
            clear.memset(tile[:].bitcast(I32), 0)
            for q in QUADRANTS:
                nc.sync.dma_start(
                    tile[QUAD * q : QUAD * q + 4, :, :].bitcast(I32),
                    src[:, 4 * q : 4 * q + 4, :].rearrange("a r c -> r a c").bitcast(I32),
                )
            return tile

        def load_channels(src, name):
            tile = held([P, PASSES, PACK], F32, name)
            nc.sync.dma_start(tile[:], src.rearrange("(b p t) -> p b t", b=PASSES, t=PACK))
            return tile

        def load_weight(src, a, b, tag):
            tile = shared([P, PACK, KP], F32, tag)
            nc.sync.dma_start(
                tile[:], src[KP * a : KP * (a + 1), KP * b : KP * (b + 1)].rearrange("(p j) c -> p j c", j=PACK)
            )
            return tile

        def load_page(b, t, tag):
            tile = shared([P, T2], F32, tag)
            nc.sync.dma_start(tile[:], page0.rearrange("(b p t) s -> b t p s", b=PASSES, t=PACK)[b, t])
            return tile

        def load_wg1(t0, t1, tag):
            tile = shared([P, t1 - t0, S], F32, tag)
            rows = wg1.rearrange("(q t) s -> q t s", t=PACK)[:, t0:t1, :]
            for q in QUADRANTS:
                nc.sync.dma_start(tile[QUAD * q : QUAD * (q + 1), :, :], rows)
            return [tile[:, t - t0, :] for t in range(t0, t1)]

        def quantize(src, codes, scales):
            nc.vector.quantize_mx(out=codes.bitcast(FP8X4), scales=scales, in_=src)
            return codes, scales

        def mx_tiles(width, tag, bufs):
            return shared([P, width], U32, tag + "_codes", bufs)[:], shared([P, width], U8, tag + "_scales", bufs)[:]

        def round_weight(raw):
            dst = grouped(KP)
            nc.scalar.copy(
                dst.rearrange("p (t m j) -> p m j t", t=PACK, j=PACK),
                raw[:].rearrange("p j (m t) -> p m j t", t=PACK),
            )
            return dst

        def interleave(copy, dst, slices):
            copy(
                dst.rearrange("p (c i t) -> p c t i", i=4, t=PACK),
                slices.rearrange("p t (c i) -> p c t i", i=4),
            )
            return dst

        def product(acc, stationary, moving):
            for a in range(PASSES):
                nc.tensor.matmul_mx(
                    out=acc, lhsT=stationary[a][0], lhsT_scale=stationary[a][1], rhs=moving[a][0],
                    rhs_scale=moving[a][1], start=(a == 0), stop=(a == PASSES - 1),
                )

        def columns(weight, b, t):
            cols = slice(P * t, P * (t + 1))
            return [(weight[a, b][0][:, cols].bitcast(FP8X4), weight[a, b][1][:, cols]) for a in range(PASSES)]

        tab2_w, tab_w, w1_raw, w3_raw, page = {}, {}, {}, {}, {}
        idx2 = load_list(offs2, "idx2")
        wg2_rows = shared([P, S], F32, "tanh", 2)
        nc.sync.dma_start(wg2_rows[:], wg2)
        tab2_w[0] = load_words(staged([P, tab2_words.shape[2]], I32), tab2_words[0])
        w2_raw = staged([P, PASSES, 2 * H], U8)
        nc.sync.dma_start(w2_raw[:].bitcast(I32), w2_words.rearrange("a p c -> p a c").bitcast(I32))
        tab2_w[1] = load_words(staged([P, tab2_words.shape[2]], I32), tab2_words[1])
        tab2_s = load_scales(tab2_scales, "tab2_s", nc.gpsimd)
        w1_raw[0, 0] = load_weight(w1, 0, 0, "big0")
        w2_raw_s = load_scales(w2_scales, "w2_raw_s", nc.vector)
        w1_raw[1, 0] = load_weight(w1, 1, 0, "big1")
        fg_t = load_channels(fg, "fg_t")
        idx1 = load_list(offs, "idx1")
        zero = held([P, 2], F32, "zero")
        nc.gpsimd.memset(zero[:, 0:1], 0.0)
        nc.scalar.activation(zero[:, 1:2], zero[:, 0:1], ACT.Gelu_apprx_tanh)
        tab_s = shared([P, tab_scales.shape[2]], U8, "tab_s")
        nc.gpsimd.memset(tab_s[:].bitcast(I32), 0)
        for q in QUADRANTS:
            nc.sync.dma_start(
                tab_s[QUAD * q : QUAD * q + 4 * PASSES, :].bitcast(I32), tab_scales[:, 4 * q : 4 * q + 4, :].bitcast(I32)
            )
        tab_w[0] = load_words(shared([P, tab_words.shape[2]], I32, "big2"), tab_words[0])
        sg_t = load_channels(sg, "sg_t")
        tab_w[1] = load_words(shared([P, tab_words.shape[2]], I32, "big3"), tab_words[1])
        page[0, 0] = load_page(0, 0, "big4")
        idx3 = load_list(offs3, "idx3")
        wg1_t = load_wg1(0, 1, "wg1_0")
        w3_raw[0, 0] = load_weight(w3, 0, 0, "big5")
        w3_raw[1, 0] = load_weight(w3, 1, 0, "big7")
        wg1_t = wg1_t + load_wg1(1, 2, "wg1_1")
        page[0, 1] = load_page(0, 1, "big6")
        idx4 = load_list(offs4, "idx4")
        idx5 = load_list(offs5, "idx5")
        pv_t = load_channels(pv, "pv_t")
        page[0, 2] = load_page(0, 2, "big8")
        wg1_t = wg1_t + load_wg1(2, PACK, "wg1_23")
        w1_raw[0, 1] = load_weight(w1, 0, 1, "big9")

        ident = held([P, P], F32, "ident")
        make_identity(nc, ident[:])
        blocks = S // P
        turned = f_bank([P, blocks, P])
        for jb in range(blocks):
            nc.tensor.transpose(turned[:, jb, :], wg2_rows[:, P * jb : P * (jb + 1)], ident[:])
        spread = shared([P, blocks, PACK, P // QUAD, QUAD], F32, "slices")
        nc.scalar.copy(
            spread[:],
            turned[:].rearrange("p b (q t) -> p b t q", t=PACK).unsqueeze(3).to_broadcast(list(spread[:].shape)),
        )
        wg2_t = held([P, PACK, S], F32, "wg2_t")
        for t in range(PACK):
            back = f_bank([P, blocks, P])
            for jb in range(blocks):
                nc.tensor.transpose(back[:, jb, :], spread[:, jb, t].rearrange("p g q -> p (g q)"), ident[:])
            nc.scalar.copy(wg2_t[:, t, :], back[:].rearrange("p b j -> p (b j)"))

        v2 = [shared([P, S], U32, "v2", PASSES) for a in range(PASSES)]
        v2_s = [held([P, S], U8, "v2_s%d" % a) for a in range(PASSES)]
        w2_w = [held([P, 2 * H], U8, "w2_w%d" % a) for a in range(PASSES)]
        w2_s = held([P, PASSES, H], U8, "w2_s")
        for a in range(PASSES):
            nc.vector.tensor_copy(v2[a][:], tab2_w[a][:].bitcast(U32).indirect(idx2[:]))
            nc.vector.tensor_copy(
                w2_w[a][:].bitcast(U16).rearrange("p (b t q) -> p b t q", b=PASSES, t=PACK),
                w2_raw[:, a, :].bitcast(U16).rearrange("p (b q t) -> p b t q", b=PASSES, t=PACK),
            )
            nc.vector.tensor_copy(v2_s[a][:], tab2_s[:, a, :].indirect(idx2[:]))
        nc.vector.tensor_copy(
            w2_s[:].rearrange("p a (b t q) -> p (a b) t q", b=PASSES, t=PACK),
            w2_raw_s[:].rearrange("p a (b q t) -> p (a b) t q", b=PASSES, t=PACK),
        )

        w1_s0 = shared([P, PASSES, KP], U8, "w2_raw_s")
        w1_q = {}
        for a in range(PASSES):
            w1_q[a, 0] = quantize(round_weight(w1_raw[a, 0]), shared([P, KP], U32, "w1_codes", 4)[:], w1_s0[:, a, :])
        v = [held([P, S], U32, "v%d" % a) for a in range(PASSES)]
        v_s = held([P, S], U8, "v_s")
        nc.vector.tensor_copy(v_s[:], tab_s[:].indirect(idx1[:]))
        for a in range(PASSES):
            nc.vector.tensor_copy(v[a][:], tab_w[a][:].bitcast(U32).indirect(idx1[:]))
        v_mx = [(v[a][:].bitcast(FP8X4), v_s[4 * a : P, :]) for a in range(PASSES)]

        w1_raw[1, 1] = load_weight(w1, 1, 1, "big0")
        page[0, 3] = load_page(0, 3, "big1")
        w3_raw[0, 1] = load_weight(w3, 0, 1, "big2")

        h1 = {}

        def make_h1(b, t, dst):
            acc = step_bank([P, S])
            product(acc[:], columns(w1_q, b, t), v_mx)
            nc.scalar.activation(dst, acc[:], ACT.Square)
            nc.scalar.activation(dst, dst, ACT.Copy, scale=sg_t[:, b, t : t + 1])
            h1[b, t] = dst

        def put_h1(b, t):
            nc.vector.tensor_tensor(page[b, t][:].indirect(idx3[:]), h1[b, t], wg1_t[t], MULT)

        def h1_tile():
            return shared([P, S], F32, "h1", PACK)[:]

        make_h1(0, 0, shared([P, S], F32, "first_h1")[:])
        put_h1(0, 0)

        after_first = shared([P, 3 * S], F32, "first_h1")
        tf_slices = shared([P, PASSES, PACK, S], BF16, "slices")
        v2_mx = [(v2[a][:].bitcast(FP8X4), v2_s[a][:]) for a in range(PASSES)]
        fw = {}
        tf_mx = []
        for b in range(PASSES):
            for t in range(PACK):
                acc = f_bank([P, S])
                c0 = KP * b + P * t
                w2_cols = [
                    (w2_w[a][:, 2 * c0 : 2 * (c0 + P)].bitcast(FP4X4), w2_s[:, a, c0 : c0 + P]) for a in range(PASSES)
                ]
                product(acc[:], w2_cols, v2_mx)
                th = shared([P, S], F32, "tanh", 2)
                nc.scalar.activation(th[:], acc[:], ACT.Tanh, bias=zero[:, 1:2])
                last = (b, t) == (PASSES - 1, PACK - 1)
                fw[b, t] = after_first[:, :S] if last else shared([P, S], F32, "fw%d%d" % (b, t))[:]
                nc.vector.tensor_tensor(fw[b, t], acc[:], wg2_t[:, t, :], MULT)
                nc.scalar.activation(tf_slices[:, b, t, :], th[:], ACT.Copy, scale=fg_t[:, b, t : t + 1])
            dst = after_first[:, S:].bitcast(BF16) if b else shared([P, PACK * S], BF16, "big3")[:]
            codes, scales = quantize(interleave(nc.vector.tensor_copy, dst, tf_slices[:, b]), *mx_tiles(S, "tf", PASSES))
            tf_mx.append((codes.bitcast(FP8X4), scales))
            if b == 0:
                make_h1(0, 1, h1_tile())
                put_h1(0, 1)

        w3_raw[1, 1] = load_weight(w3, 1, 1, "big3")
        w4_s = load_scales(w4_scales, "tab_s", nc.gpsimd)
        w4_w = [load_words(shared([P, N], I32, "v2", PASSES), w4_words[a]) for a in range(PASSES)]

        g = {}

        def make_g(b, t):
            acc = step_bank([P, S])
            product(acc[:], columns(w3_q, b, t), tf_mx)
            g[b, t] = shared([P, S], F32, "g", PACK)
            nc.scalar.copy(g[b, t][:], acc[:])

        def put_h2(b, t):
            nc.vector.tensor_tensor(page[b, t][:].indirect(idx4[:]), g[b, t][:], fw[b, t], MULT)

        w3_q = {}
        for a in range(PASSES):
            w3_q[a, 0] = quantize(round_weight(w3_raw[a, 0]), *mx_tiles(KP, "w3", 2 * PASSES))
        page[1, 0] = load_page(1, 0, "big5")
        page[1, 1] = load_page(1, 1, "big7")
        for t in range(PACK):
            make_g(0, t)
        for t in range(2, PACK):
            make_h1(0, t, h1_tile())
        for a in range(PASSES):
            w1_q[a, 1] = quantize(
                round_weight(w1_raw[a, 1]), shared([P, KP], U32, "w1_codes", 4)[:],
                shared([P, KP], U8, "w1_scales", PASSES)[:],
            )
        page[1, 2] = load_page(1, 2, "big9")
        page[1, 3] = load_page(1, 3, "big0")
        for a in range(PASSES):
            w3_q[a, 1] = quantize(round_weight(w3_raw[a, 1]), *mx_tiles(KP, "w3", 2 * PASSES))
        h1_second = shared([P, PACK, S], F32, "big3")
        for t in range(PACK):
            make_h1(1, t, h1_second[:, t, :])

        def fetch(b, t, c0, width):
            picked = staged([P, width], F32)
            nc.vector.tensor_copy(
                picked[:], page[b, t][:].indirect(idx5[:, c0 // LIST_ROWS : (c0 + width) // LIST_ROWS])
            )
            return picked

        def add_pv(b, t, dst, picked):
            nc.scalar.activation(dst, picked, ACT.Identity, bias=pv_t[:, b, t : t + 1])

        x_first = shared([P, PACK, PJ], BF16, "big2")
        for t in range(PACK):
            if t >= 2:
                put_h1(0, t)
            put_h2(0, t)
            make_g(1, t)
            add_pv(0, t, x_first[:, t, :], fetch(0, t, 0, PJ)[:])
        halves = PJ // S
        x_grouped = [interleave(nc.scalar.copy, grouped(S), x_first[:, :, S * h : S * (h + 1)]) for h in range(halves)]

        x_second = shared([P, PACK, PJ], BF16, "big2")
        chunks = PJ // CH
        acc_y = {}

        def y_pass(a, c, codes, scales):
            for n in range(N // P):
                pair, side = divmod(n, 2)
                nc.tensor.matmul_mx(
                    out=acc_y[c, pair][:, side, :], lhsT=w4_w[a][:, P * n : P * (n + 1)].bitcast(FP8X4),
                    lhsT_scale=w4_s[:, a, P * n : P * (n + 1)], rhs=codes.bitcast(FP8X4), rhs_scale=scales,
                    start=(a == 0 and side == 0), stop=(a == PASSES - 1 and side == 1),
                )

        for t in range(PACK):
            put_h1(1, t)
            put_h2(1, t)
            if t < halves:
                codes, scales = quantize(
                    x_grouped[t], shared([P, S], U32, "fw1%d" % t)[:], shared([P, S], U8, "x0_scales", halves)[:]
                )
                for cc in range(S // CH):
                    c = (S // CH) * t + cc
                    for pair in range(2):
                        acc_y[c, pair] = (step_bank if c == chunks - 1 else f_bank)([P, 2, CH])
                    y_pass(0, c, codes[:, CH * cc : CH * (cc + 1)], scales[:, CH * cc : CH * (cc + 1)])
            if t < PACK - 1:
                add_pv(1, t, x_second[:, t, :], fetch(1, t, 0, PJ)[:])

        t = PACK - 1
        for h in range(halves):
            picked = fetch(1, t, S * h, S)
            for cc in range(S // CH):
                c0 = S * h + CH * cc
                add_pv(1, t, x_second[:, t, c0 : c0 + CH], picked[:, CH * cc : CH * (cc + 1)])
        for c in range(chunks):
            cols = slice(CH * c, CH * (c + 1))
            words = interleave(nc.vector.tensor_copy, grouped(CH), x_second[:, :, cols])
            y_pass(1, c, *quantize(words, *mx_tiles(CH, "x1", chunks)))
            for pair in range(2):
                res = shared([P, 2, CH], F32, ("h1", "g")[pair], PACK)
                nc.scalar.activation(res[:], acc_y[c, pair][:], ACT.Gelu_apprx_tanh)
                nc.sync.dma_start(
                    out[2 * P * pair : 2 * P * (pair + 1), cols].rearrange("(n p) j -> p n j", p=P), res[:]
                )
